import numpy as np
import ml_dtypes


def mxq(x, axis, fmt="e4m3"):
    dtype, down = {"e4m3": (ml_dtypes.float8_e4m3fn, 7), "e5m2": (ml_dtypes.float8_e5m2, 14)}[fmt]
    v = np.moveaxis(np.asarray(x, np.float32).astype(ml_dtypes.bfloat16).astype(np.float64), axis, -1)
    blocks = v.reshape(v.shape[:-1] + (-1, 32))
    amax = np.abs(blocks).max(-1, keepdims=True)
    byte = np.maximum(np.where(amax > 0, np.frexp(amax)[1] - 1 + 127, 0) - down, 1)
    scale = np.exp2(byte - 127.0)
    codes = (blocks / scale).astype(np.float32).astype(dtype).astype(np.float64)
    return np.moveaxis((codes * scale).reshape(v.shape), -1, axis)


WIDE = False


def mx_kscale(k):
    if not WIDE:
        return np.ones(k)
    levels = np.array([10, -10, 5, -5, 0])
    if k % 512:
        return np.exp2(np.random.permutation(np.resize(levels, k // 32))).repeat(32)
    a = np.empty((k // 512, 16))
    for p in range(k // 512):
        a[p, :8] = np.random.permutation(np.resize(levels, 8))
        for g in range(8):
            far = levels[np.abs(levels - a[p, g]) >= 10]
            a[p, g + 8] = far[np.random.randint(len(far))]
    return np.exp2(a.ravel()).repeat(32)


def f64(x):
    return np.asarray(x).astype(np.float64)


def striped(idx):
    return np.tile(idx.reshape(-1, 16).T, (8, 1)).astype(np.uint16)


def unstriped(offs):
    return offs[:16].T.reshape(-1).astype(np.int64)


def pack_weight(w):
    k, n = w.shape
    w = f64(np.asarray(w, np.float32).astype(ml_dtypes.bfloat16)).reshape(k // 32, 32, n)
    amax = np.abs(w).max(1)
    byte = np.clip(np.where(amax > 0, np.frexp(amax)[1] - 1 + 127 - 7, 1), 1, 254)
    scaled = (w * np.exp2(127.0 - byte)[:, None, :]).reshape(k, n).astype(np.float32)
    words = np.ascontiguousarray(scaled.reshape(k // 512, 128, 4, n).transpose(0, 1, 3, 2)).astype(ml_dtypes.float8_e4m3fn).view(np.uint8)
    return words, np.ascontiguousarray(byte.astype(np.uint8).reshape(k // 512, 16, n))


def unpack_weight(words, scales):
    g, p, n, _ = words.shape
    vals = np.ascontiguousarray(words).view(ml_dtypes.float8_e4m3fn).astype(np.float64) * np.repeat(np.exp2(scales.astype(np.float64) - 127.0), 8, axis=1)[..., None]
    return vals.transpose(0, 1, 3, 2).reshape(g * 512, n)


def planes(y):
    n, m = y.shape
    v = y.astype(np.float32).astype(ml_dtypes.bfloat16).astype(np.float64).reshape(n // 32, 32, m)
    top = np.abs(v).max(1)
    byte = np.clip(np.where(top > 0, np.frexp(top)[1] - 1 + 127 - 7, 1), 1, 254)
    codes = (v * np.exp2(127.0 - byte)[:, None, :]).reshape(n, m).astype(np.float32).astype(ml_dtypes.float8_e4m3fn).view(np.uint8)
    words = codes.reshape(n // 512, 128, 4, m).transpose(0, 1, 3, 2)
    return np.ascontiguousarray(words), np.ascontiguousarray(byte.astype(np.uint8).reshape(n // 512, 16, m))


def relu(v):
    return np.maximum(v, 0.0)


def sigmoid(v):
    return 1.0 / (1.0 + np.exp(-np.maximum(v, -700.0)))


K, T, S, V, N = 512, 4096, 1024, 512, 512


def setup_inputs():
    n = np.random.standard_normal
    s = mx_kscale(K)[:, None]
    near = np.random.permutation(S)
    packed_xT = pack_weight(n((K, T)) * s)
    return {
        "x_words": packed_xT[0],
        "x_scales": packed_xT[1],
        "w0": (n((K, N)) / np.sqrt(K) / s).astype(np.float32),
        "w1": (n((K, N)) / np.sqrt(K) / s).astype(np.float32),
        "w2": (n((K, N)) / np.sqrt(K) / s).astype(np.float32),
        "offs": striped(np.random.permutation(T)[:S]),
        "cen": striped(np.random.permutation(S)[:V]),
        "pos1": striped(near[:V]),
        "pos2": striped(near[V:]),
    }


def reference(x_words, x_scales, w0, w1, w2, offs, cen, pos1, pos2):
    xq = unpack_weight(x_words, x_scales)[:, unstriped(offs)]
    m0 = sigmoid(mxq(f64(w1), 0, "e4m3").T @ xq)
    c0 = m0[:, unstriped(cen)]
    y = mxq(f64(w0), 0, "e4m3").T @ xq
    m1 = sigmoid(mxq(f64(w2), 0, "e4m3").T @ xq)
    c1 = m1[:, unstriped(cen)]
    out_0 = relu(c0 * y[:, unstriped(pos1)] + c1 * y[:, unstriped(pos2)])
    return (out_0,) + planes(out_0)

@@ -1,0 +1,230 @@
+from contextlib import ExitStack
+
+import concourse.mybir as mybir
+from concourse.masks import make_identity
+
+K, T, S, V, N = 512, 4096, 1024, 512, 512
+FLOPS = 3 * 2 * K * N * S
+
+F32 = mybir.dt.float32
+BF16 = mybir.dt.bfloat16
+I32 = mybir.dt.int32
+U32 = mybir.dt.uint32
+U16 = mybir.dt.uint16
+U8 = mybir.dt.uint8
+FP8X4 = mybir.dt.float8_e4m3fn_x4
+ACT = mybir.ActivationFunctionType
+ALU = mybir.AluOpType
+
+P = 128
+PACK = 4
+HALF = 512
+
+
+def tile_picked_zmodd_relu_po_kernel(tc, x_words, x_scales, w0, w1, w2, offs, cen, pos1, pos2, out_0, out_1, out_2):
+    nc = tc.nc
+    with ExitStack() as ctx:
+        keep = ctx.enter_context(tc.tile_pool(name="keep", bufs=1))
+        psum = ctx.enter_context(tc.psum_pool(name="psum", bufs=1))
+
+        offs_t = keep.tile([P, S // 16], U16, name="offs_t")
+        cen_t = keep.tile([P, V // 16], U16, name="cen_t")
+        pos1_t = keep.tile([P, V // 16], U16, name="pos1_t")
+        pos2_t = keep.tile([P, V // 16], U16, name="pos2_t")
+        xw = keep.tile([P, T], U32, name="xw", align_bytes=64)
+        xs = keep.tile([P, T], U8, name="xs", align_bytes=64)
+        raw = [keep.tile([P, PACK, N], F32, name="raw%d" % i, align_bytes=64) for i in range(3)]
+        grp = [keep.tile([P, PACK * N], BF16, name="grp%d" % i, align_bytes=64) for i in range(3)]
+        wc = [keep.tile([P, N], U32, name="wc%d" % i, align_bytes=64) for i in range(3)]
+        ws = [keep.tile([P, N], U8, name="ws%d" % i, align_bytes=64) for i in range(3)]
+        warm = keep.tile([P, 1], F32, name="warm")
+        warm2 = keep.tile([P, 1], F32, name="warm2")
+        ident = keep.tile([P, P], F32, name="ident")
+        gs0 = keep.tile([P, S], U8, name="gs0", align_bytes=64)
+        gs = keep.tile([P, S], U8, name="gs", align_bytes=64)
+        gw = [keep.tile([P, HALF], U32, name="gw%d" % h, align_bytes=64) for h in range(2)]
+        rows = [[keep.tile([P, S], F32, name="rows%d_%d" % (i, t)) for t in range(PACK)] for i in range(3)]
+        yg = [[None] * PACK for d in range(2)]
+        slot = (0, 1, 0, 0)
+        pr = [[keep.tile([P, V], F32, name="pr%d_%d" % (d, t)) for t in range(PACK)] for d in range(2)]
+        turned = [keep.tile([P, V], F32, name="turned%d" % t) for t in range(PACK)]
+        two = [keep.tile([P, 2, V], F32, name="two%d" % u) for u in range(2)]
+        og = keep.tile([P, V, PACK], BF16, name="og", align_bytes=64)
+        oc = keep.tile([P, V], U32, name="oc", align_bytes=64)
+        osc = keep.tile([P, V], U8, name="osc", align_bytes=64)
+        out_rows = out_0.rearrange("(p t) c -> p t c", t=PACK)
+        pos_t = (pos1_t, pos2_t)
+
+        def load_w(i, w):
+            nc.sync.dma_start(out=raw[i][:], in_=w.rearrange("(p j) c -> p j c", j=PACK))
+
+        def load_scales(eng):
+            eng.dma_start(out=xs[0:P:8, :].bitcast(I32), in_=x_scales[0].bitcast(I32))
+
+        def load_scales4(eng):
+            for q in range(4):
+                eng.dma_start(out=xs[32 * q : 32 * q + 4, :].bitcast(I32), in_=x_scales[0, 4 * q : 4 * q + 4, :].bitcast(I32))
+
+        def load_x():
+            nc.sync.dma_start(out=xw[:].bitcast(I32), in_=x_words[0].rearrange("p n t -> p (n t)").bitcast(I32))
+
+        def deal(i, eng, m0=0, m1=P):
+            o = grp[i][:].rearrange("p (t m j) -> p m j t", t=PACK, j=PACK)[:, m0:m1]
+            s = raw[i][:].rearrange("p j (m t) -> p m j t", t=PACK)[:, m0:m1]
+            if eng == "v":
+                nc.vector.tensor_copy(out=o, in_=s)
+            elif eng == "g":
+                nc.gpsimd.tensor_scalar(o, s, 1.0, 0.0, ALU.mult, ALU.add)
+            else:
+                nc.scalar.copy(out=o, in_=s)
+
+        def quant(i, t0=0, t1=PACK):
+            nc.vector.quantize_mx(out=wc[i][:, P * t0 : P * t1].bitcast(FP8X4), scales=ws[i][:, P * t0 : P * t1], in_=grp[i][:, N * t0 : N * t1])
+
+        def gscales(eng):
+            nc.vector.tensor_copy(gs0[:], xs[:].indirect(offs_t[:]))
+            nc.vector.tensor_copy(gs[:].bitcast(I32), gs0[:].bitcast(I32))
+            for r in range(1, 4):
+                eng.dma_start(out=gs[r:P:32, :].bitcast(I32), in_=gs0[8 * r : P : 32, :].bitcast(I32))
+
+        def gscales4():
+            nc.vector.tensor_copy(gs[:], xs[:].indirect(offs_t[:]))
+
+        def gwords(h):
+            nc.vector.tensor_copy(gw[h][:], xw[:].indirect(offs_t[:, 32 * h : 32 * h + 32]))
+
+        def product(i, t, h, b, eng="s"):
+            acc = psum.tile([P, HALF], F32, name="bank%d" % b)
+            cols = slice(P * t, P * t + P)
+            nc.tensor.matmul_mx(out=acc[:], lhsT=wc[i][:, cols].bitcast(FP8X4), lhsT_scale=ws[i][:, cols],
+                                rhs=gw[h][:].bitcast(FP8X4), rhs_scale=gs[:, HALF * h : HALF * h + HALF], start=True, stop=True)
+            dst = rows[i][t][:, HALF * h : HALF * h + HALF]
+            if eng == "v":
+                nc.vector.tensor_copy(out=dst, in_=acc[:])
+            elif i == 0:
+                nc.scalar.copy(out=dst, in_=acc[:])
+            else:
+                nc.scalar.activation(out=dst, in_=acc[:], func=ACT.Sigmoid)
+
+        def both(i, t, b):
+            product(i, t, 0, b)
+            product(i, t, 1, b + 1)
+
+        def gy(d, t):
+            yg[d][t] = keep.tile([P, V], F32, name="yg%d_%d" % (d, slot[t]))
+            nc.vector.tensor_copy(yg[d][t][:], rows[0][t][:].indirect(pos_t[d][:]))
+
+        def fused(d, t, a=0, b=V):
+            nc.vector.tensor_tensor(pr[d][t][:, a:b], rows[1 + d][t][:].indirect(cen_t[:, a // 16 : b // 16]), yg[d][t][:, a:b], ALU.mult)
+
+        def pe_add(t, b):
+            bank = psum.tile([P, V], F32, name="bank%d" % b)
+            for c in range(0, V, P):
+                for d in range(2):
+                    nc.tensor.matmul(bank[:, c : c + P], lhsT=pr[d][t][:, c : c + P], rhs=ident[:], is_transpose=True, start=(d == 0), stop=(d == 1))
+            nc.scalar.activation(out=turned[t][:], in_=bank[:], func=ACT.Relu)
+
+        def pe_back(t, b):
+            bank = psum.tile([P, V], F32, name="bank%d" % b)
+            for c in range(0, V, P):
+                nc.tensor.transpose(bank[:, c : c + P], turned[t][:, c : c + P], ident[:])
+            nc.scalar.copy(out=two[t // 2][:, t % 2, :], in_=bank[:])
+            nc.sync.dma_start(out=out_rows[:, t, :], in_=two[t // 2][:, t % 2, :])
+
+        def addv(t, a, b, eng=nc.vector):
+            eng.tensor_tensor(two[t // 2][:, t % 2, a:b], pr[0][t][:, a:b], pr[1][t][:, a:b], ALU.add)
+
+        def store(t, a, b):
+            dst = keep.tile([P, V], F32, name="turned2")
+            nc.scalar.activation(out=dst[:, a:b], in_=two[t // 2][:, t % 2, a:b], func=ACT.Relu)
+            nc.sync.dma_start(out=out_rows[:, t, a:b], in_=dst[:, a:b])
+
+        def pair(u, a, b, eng):
+            o = og[:, a:b, 2 * u : 2 * u + 2]
+            s = two[u][:, :, a:b].rearrange("p t c -> p c t")
+            if eng == "s":
+                nc.scalar.activation(out=o, in_=s, func=ACT.Relu)
+            else:
+                nc.vector.tensor_scalar_max(o, s, 0.0)
+
+        def quantc(a, b):
+            nc.vector.quantize_mx(out=oc[:, a:b].bitcast(FP8X4), scales=osc[:, a:b], in_=og[:, a:b, :].rearrange("p c t -> p (c t)"))
+            nc.sync.dma_start(out=out_1[0, :, a:b, :].rearrange("p n t -> p (n t)").bitcast(I32), in_=oc[:, a:b].bitcast(I32))
+
+        def scales_out():
+            for q in range(4):
+                eng = nc.scalar if q % 2 == 0 else nc.sync
+                eng.dma_start(out=out_2[0, 4 * q : 4 * q + 4, :].bitcast(I32), in_=osc[32 * q : 32 * q + 4, :].bitcast(I32))
+
+        def clock(name, ap, dt):
+            c = keep.tile([P, 1], dt, name=name)
+            nc.gpsimd.tensor_copy(c[:], ap)
+
+        nc.vector.memset(xs[:].bitcast(I32), 0)
+        nc.vector.memset(warm[:], 0.0)
+        nc.scalar.activation(out=warm2[:], in_=warm[:], func=ACT.Sigmoid)
+        make_identity(nc, ident[:])
+        load_w(0, w0)
+        nc.sync.dma_start(offs_t[:], offs)
+        load_scales4(nc.sync)
+        load_x()
+        nc.sync.dma_start(pos1_t[:], pos1)
+        load_w(1, w1)
+        nc.sync.dma_start(pos2_t[:], pos2)
+        load_w(2, w2)
+        nc.sync.dma_start(cen_t[:], cen)
+        deal(0, "v")
+        quant(0)
+        gscales4()
+        gwords(0)
+        gwords(1)
+        product(0, 0, 0, 0)
+        product(0, 1, 0, 1)
+        product(0, 0, 1, 2)
+        product(0, 1, 1, 3)
+        deal(1, "v")
+        gy(0, 0)
+        quant(1)
+        deal(2, "s")
+        gy(1, 0)
+        both(1, 0, 4)
+        gy(0, 1)
+        quant(2)
+        gy(1, 1)
+        both(2, 0, 6)
+        both(1, 1, 0)
+        both(0, 2, 4)
+        both(2, 1, 6)
+        both(1, 2, 0)
+        both(2, 2, 2)
+        both(0, 3, 4)
+        both(1, 3, 6)
+        both(2, 3, 0)
+        fused(0, 0)
+        fused(1, 0)
+        fused(0, 1)
+        gy(0, 2)
+        fused(1, 1)
+        gy(1, 2)
+        fused(0, 2)
+        fused(1, 2)
+        gy(0, 3)
+        gy(1, 3)
+        pe_add(0, 2)
+        pe_add(1, 3)
+        pe_back(0, 4)
+        pe_back(1, 5)
+        pe_add(2, 6)
+        pe_back(2, 7)
+        pair(0, 0, V, "s")
+        fused(0, 3)
+        fused(1, 3, 0, 256)
+        fused(1, 3, 256, 512)
+        addv(3, 0, 256)
+        pair(1, 0, 256, "s")
+        addv(3, 256, 512)
+        store(3, 0, 512)
+        pair(1, 256, 512, "v")
+        quantc(256, 512)
+        quantc(0, 256)
+        scales_out()

@@ -33,8 +33,8 @@ def tile_picked_zmodd_relu_po_kernel(tc, x_words, x_scales, w0, w1, w2, offs, ce
         pos2_t = keep.tile([P, V // 16], U16, name="pos2_t")
         xw = keep.tile([P, T], U32, name="xw", align_bytes=64)
         xs = keep.tile([P, T], U8, name="xs", align_bytes=64)
-        raw = [keep.tile([P, PACK, N], F32, name="raw%d" % i, align_bytes=64) for i in range(3)]
-        grp = [keep.tile([P, PACK * N], BF16, name="grp%d" % i, align_bytes=64) for i in range(3)]
+        raw = [None] * 3
+        grp = [None] * 3
         wc = [keep.tile([P, N], U32, name="wc%d" % i, align_bytes=64) for i in range(3)]
         ws = [keep.tile([P, N], U8, name="ws%d" % i, align_bytes=64) for i in range(3)]
         warm = keep.tile([P, 1], F32, name="warm")
@@ -43,12 +43,12 @@ def tile_picked_zmodd_relu_po_kernel(tc, x_words, x_scales, w0, w1, w2, offs, ce
         gs0 = keep.tile([P, S], U8, name="gs0", align_bytes=64)
         gs = keep.tile([P, S], U8, name="gs", align_bytes=64)
         gw = [keep.tile([P, HALF], U32, name="gw%d" % h, align_bytes=64) for h in range(2)]
-        rows = [[keep.tile([P, S], F32, name="rows%d_%d" % (i, t)) for t in range(PACK)] for i in range(3)]
+        rows = [[keep.tile([P, S], F32, name="rows%d_%d" % (i, t), align_bytes=64) for t in range(PACK)] for i in range(3)]
         yg = [[None] * PACK for d in range(2)]
         slot = (0, 1, 0, 0)
-        pr = [[keep.tile([P, V], F32, name="pr%d_%d" % (d, t)) for t in range(PACK)] for d in range(2)]
+        pr = [None, [keep.tile([P, V], F32, name="pr1_%d" % t)[:] for t in range(PACK)]]
         turned = [keep.tile([P, V], F32, name="turned%d" % t) for t in range(PACK)]
-        two = [keep.tile([P, 2, V], F32, name="two%d" % u) for u in range(2)]
+        res = keep.tile([P, PACK, V], F32, name="res")
         og = keep.tile([P, V, PACK], BF16, name="og", align_bytes=64)
         oc = keep.tile([P, V], U32, name="oc", align_bytes=64)
         osc = keep.tile([P, V], U8, name="osc", align_bytes=64)
@@ -56,6 +56,7 @@ def tile_picked_zmodd_relu_po_kernel(tc, x_words, x_scales, w0, w1, w2, offs, ce
         pos_t = (pos1_t, pos2_t)
 
         def load_w(i, w):
+            raw[i] = keep.tile([P, PACK, N], F32, name=("raw0", "raw1", "xw")[i], align_bytes=64)
             nc.sync.dma_start(out=raw[i][:], in_=w.rearrange("(p j) c -> p j c", j=PACK))
 
         def load_scales(eng):
@@ -69,8 +70,10 @@ def tile_picked_zmodd_relu_po_kernel(tc, x_words, x_scales, w0, w1, w2, offs, ce
             nc.sync.dma_start(out=xw[:].bitcast(I32), in_=x_words[0].rearrange("p n t -> p (n t)").bitcast(I32))
 
         def deal(i, eng, m0=0, m1=P):
-            o = grp[i][:].rearrange("p (t m j) -> p m j t", t=PACK, j=PACK)[:, m0:m1]
-            s = raw[i][:].rearrange("p j (m t) -> p m j t", t=PACK)[:, m0:m1]
+            if m0 == 0:
+                grp[i] = keep.tile([P, PACK * N], BF16, name=("grp0", "grp1", "rows0_0")[i], align_bytes=64)
+            o = grp[i][:].rearrange("p (t m j) -> p m t j", t=PACK, j=PACK)[:, m0:m1]
+            s = raw[i][:].rearrange("p j (m t) -> p m t j", t=PACK)[:, m0:m1]
             if eng == "v":
                 nc.vector.tensor_copy(out=o, in_=s)
             elif eng == "g":
@@ -83,9 +86,8 @@ def tile_picked_zmodd_relu_po_kernel(tc, x_words, x_scales, w0, w1, w2, offs, ce
 
         def gscales(eng):
             nc.vector.tensor_copy(gs0[:], xs[:].indirect(offs_t[:]))
-            nc.vector.tensor_copy(gs[:].bitcast(I32), gs0[:].bitcast(I32))
-            for r in range(1, 4):
-                eng.dma_start(out=gs[r:P:32, :].bitcast(I32), in_=gs0[8 * r : P : 32, :].bitcast(I32))
+            for q in range(4):
+                eng.dma_start(out=gs[32 * q : 32 * q + 4, :].bitcast(I32), in_=gs0[32 * q : 32 * q + 32 : 8, :].bitcast(I32))
 
         def gscales4():
             nc.vector.tensor_copy(gs[:], xs[:].indirect(offs_t[:]))
@@ -111,8 +113,16 @@ def tile_picked_zmodd_relu_po_kernel(tc, x_words, x_scales, w0, w1, w2, offs, ce
             product(i, t, 1, b + 1)
 
         def gy(d, t):
-            yg[d][t] = keep.tile([P, V], F32, name="yg%d_%d" % (d, slot[t]))
-            nc.vector.tensor_copy(yg[d][t][:], rows[0][t][:].indirect(pos_t[d][:]))
+            nc.vector.tensor_copy(yg[d][t], rows[0][t][:].indirect(pos_t[d][:]))
+
+        def open_yg(name, items):
+            held = keep.tile([P, len(items), V], F32, name=name, align_bytes=64)
+            for k, (d, t) in enumerate(items):
+                yg[d][t] = held[:, k, :]
+
+        def open_pr0():
+            first = keep.tile([P, PACK, V], F32, name="xw", align_bytes=64)
+            pr[0] = [first[:, t, :] for t in range(PACK)]
 
         def fused(d, t, a=0, b=V):
             nc.vector.tensor_tensor(pr[d][t][:, a:b], rows[1 + d][t][:].indirect(cen_t[:, a // 16 : b // 16]), yg[d][t][:, a:b], ALU.mult)
@@ -128,20 +138,19 @@ def tile_picked_zmodd_relu_po_kernel(tc, x_words, x_scales, w0, w1, w2, offs, ce
             bank = psum.tile([P, V], F32, name="bank%d" % b)
             for c in range(0, V, P):
                 nc.tensor.transpose(bank[:, c : c + P], turned[t][:, c : c + P], ident[:])
-            nc.scalar.copy(out=two[t // 2][:, t % 2, :], in_=bank[:])
-            nc.sync.dma_start(out=out_rows[:, t, :], in_=two[t // 2][:, t % 2, :])
+            nc.scalar.copy(out=res[:, t, :], in_=bank[:])
+            nc.sync.dma_start(out=out_rows[:, t, :], in_=res[:, t, :])
 
         def addv(t, a, b, eng=nc.vector):
-            eng.tensor_tensor(two[t // 2][:, t % 2, a:b], pr[0][t][:, a:b], pr[1][t][:, a:b], ALU.add)
+            eng.tensor_tensor(res[:, t, a:b], pr[0][t][:, a:b], pr[1][t][:, a:b], ALU.add)
 
-        def store(t, a, b):
-            dst = keep.tile([P, V], F32, name="turned2")
-            nc.scalar.activation(out=dst[:, a:b], in_=two[t // 2][:, t % 2, a:b], func=ACT.Relu)
+        def store(t, dst, a, b):
+            nc.scalar.activation(out=dst[:, a:b], in_=res[:, t, a:b], func=ACT.Relu)
             nc.sync.dma_start(out=out_rows[:, t, a:b], in_=dst[:, a:b])
 
-        def pair(u, a, b, eng):
-            o = og[:, a:b, 2 * u : 2 * u + 2]
-            s = two[u][:, :, a:b].rearrange("p t c -> p c t")
+        def weave(a, b, eng):
+            o = og[:, a:b, :]
+            s = res[:, :, a:b].rearrange("p t c -> p c t")
             if eng == "s":
                 nc.scalar.activation(out=o, in_=s, func=ACT.Relu)
             else:
@@ -162,69 +171,75 @@ def tile_picked_zmodd_relu_po_kernel(tc, x_words, x_scales, w0, w1, w2, offs, ce
 
         nc.vector.memset(xs[:].bitcast(I32), 0)
         nc.vector.memset(warm[:], 0.0)
+        nc.vector.memset(gs[:].bitcast(I32), 0)
         nc.scalar.activation(out=warm2[:], in_=warm[:], func=ACT.Sigmoid)
         make_identity(nc, ident[:])
         load_w(0, w0)
         nc.sync.dma_start(offs_t[:], offs)
-        load_scales4(nc.sync)
-        load_x()
+        load_scales(nc.sync)
         nc.sync.dma_start(pos1_t[:], pos1)
+        load_x()
         load_w(1, w1)
         nc.sync.dma_start(pos2_t[:], pos2)
-        load_w(2, w2)
         nc.sync.dma_start(cen_t[:], cen)
-        deal(0, "v")
+        deal(0, "s")
+        gscales(nc.scalar)
         quant(0)
-        gscales4()
         gwords(0)
         gwords(1)
+        load_w(2, w2)
         product(0, 0, 0, 0)
         product(0, 1, 0, 1)
         product(0, 0, 1, 2)
         product(0, 1, 1, 3)
         deal(1, "v")
+        open_yg("raw1", [(0, 0)])
         gy(0, 0)
         quant(1)
-        deal(2, "s")
+        open_yg("grp1", [(1, 0), (0, 1), (1, 1), (0, 2), (1, 2)])
         gy(1, 0)
-        both(1, 0, 4)
-        gy(0, 1)
+        deal(2, "g")
         quant(2)
-        gy(1, 1)
-        both(2, 0, 6)
-        both(1, 1, 0)
-        both(0, 2, 4)
-        both(2, 1, 6)
-        both(1, 2, 0)
-        both(2, 2, 2)
+        open_pr0()
+        both(1, 0, 4)
+        both(1, 1, 6)
+        both(0, 2, 0)
+        both(1, 2, 2)
         both(0, 3, 4)
         both(1, 3, 6)
-        both(2, 3, 0)
-        fused(0, 0)
-        fused(1, 0)
-        fused(0, 1)
+        both(2, 0, 0)
+        both(2, 1, 2)
+        both(2, 2, 4)
+        both(2, 3, 6)
+        gy(0, 1)
+        gy(1, 1)
         gy(0, 2)
-        fused(1, 1)
         gy(1, 2)
+        fused(0, 0)
+        fused(0, 1)
         fused(0, 2)
+        fused(1, 0)
+        fused(1, 1)
         fused(1, 2)
+        open_yg("rows2_2", [(0, 3), (1, 3)])
         gy(0, 3)
         gy(1, 3)
-        pe_add(0, 2)
-        pe_add(1, 3)
-        pe_back(0, 4)
-        pe_back(1, 5)
-        pe_add(2, 6)
-        pe_back(2, 7)
-        pair(0, 0, V, "s")
+        pe_add(0, 0)
+        pe_add(1, 1)
+        pe_back(0, 2)
+        pe_add(2, 3)
+        pe_back(1, 4)
+        pe_back(2, 5)
         fused(0, 3)
         fused(1, 3, 0, 256)
         fused(1, 3, 256, 512)
         addv(3, 0, 256)
-        pair(1, 0, 256, "s")
+        last = keep.tile([P, V], F32, name="turned2")
+        store(3, last, 0, 256)
+        weave(0, 192, "s")
         addv(3, 256, 512)
-        store(3, 0, 512)
-        pair(1, 256, 512, "v")
+        store(3, last, 256, 512)
+        weave(192, 512, "v")
         quantc(256, 512)
         quantc(0, 256)
         scales_out()

@@ -1,7 +1,6 @@
 from contextlib import ExitStack
 
 import concourse.mybir as mybir
-from concourse.masks import make_identity
 
 K, T, S, V, N = 512, 4096, 1024, 512, 512
 FLOPS = 3 * 2 * K * N * S
@@ -19,6 +18,8 @@ ALU = mybir.AluOpType
 P = 128
 PACK = 4
 HALF = 512
+BANKS = 8
+Y, M0, M1 = 0, 1, 2
 
 
 def tile_picked_zmodd_relu_po_kernel(tc, x_words, x_scales, w0, w1, w2, offs, cen, pos1, pos2, out_0, out_1, out_2):
@@ -39,39 +40,36 @@ def tile_picked_zmodd_relu_po_kernel(tc, x_words, x_scales, w0, w1, w2, offs, ce
         ws = [keep.tile([P, N], U8, name="ws%d" % i, align_bytes=64) for i in range(3)]
         warm = keep.tile([P, 1], F32, name="warm")
         warm2 = keep.tile([P, 1], F32, name="warm2")
-        ident = keep.tile([P, P], F32, name="ident")
         gs0 = keep.tile([P, S], U8, name="gs0", align_bytes=64)
         gs = keep.tile([P, S], U8, name="gs", align_bytes=64)
         gw = [keep.tile([P, HALF], U32, name="gw%d" % h, align_bytes=64) for h in range(2)]
         rows = [[keep.tile([P, S], F32, name="rows%d_%d" % (i, t), align_bytes=64) for t in range(PACK)] for i in range(3)]
-        yg = [[None] * PACK for d in range(2)]
-        slot = (0, 1, 0, 0)
-        pr = [None, [keep.tile([P, V], F32, name="pr1_%d" % t)[:] for t in range(PACK)]]
-        turned = [keep.tile([P, V], F32, name="turned%d" % t) for t in range(PACK)]
+        mask = [[keep.tile([P, V], F32, name="mask%d_%d" % (d, t), align_bytes=64) for t in range(PACK)] for d in range(2)]
+        pr = [[None] * PACK, [keep.tile([P, V], F32, name="pr1_%d" % t)[:] for t in range(PACK)]]
         res = keep.tile([P, PACK, V], F32, name="res")
+        fin = [keep.tile([P, V], F32, name="fin%d" % t) for t in range(PACK)]
         og = keep.tile([P, V, PACK], BF16, name="og", align_bytes=64)
         oc = keep.tile([P, V], U32, name="oc", align_bytes=64)
         osc = keep.tile([P, V], U8, name="osc", align_bytes=64)
         out_rows = out_0.rearrange("(p t) c -> p t c", t=PACK)
         pos_t = (pos1_t, pos2_t)
+        weights = (w0, w1, w2)
+        accs = {}
 
-        def load_w(i, w):
-            raw[i] = keep.tile([P, PACK, N], F32, name=("raw0", "raw1", "xw")[i], align_bytes=64)
-            nc.sync.dma_start(out=raw[i][:], in_=w.rearrange("(p j) c -> p j c", j=PACK))
+        def load_w(i, name):
+            raw[i] = keep.tile([P, PACK, N], F32, name=name, align_bytes=64)
+            nc.sync.dma_start(out=raw[i][:], in_=weights[i].rearrange("(p j) c -> p j c", j=PACK))
 
         def load_scales(eng):
             eng.dma_start(out=xs[0:P:8, :].bitcast(I32), in_=x_scales[0].bitcast(I32))
 
-        def load_scales4(eng):
-            for q in range(4):
-                eng.dma_start(out=xs[32 * q : 32 * q + 4, :].bitcast(I32), in_=x_scales[0, 4 * q : 4 * q + 4, :].bitcast(I32))
-
         def load_x():
             nc.sync.dma_start(out=xw[:].bitcast(I32), in_=x_words[0].rearrange("p n t -> p (n t)").bitcast(I32))
 
+        def open_grp(i, name):
+            grp[i] = keep.tile([P, PACK * N], BF16, name=name, align_bytes=64)
+
         def deal(i, eng, m0=0, m1=P):
-            if m0 == 0:
-                grp[i] = keep.tile([P, PACK * N], BF16, name=("grp0", "grp1", "rows0_0")[i], align_bytes=64)
             o = grp[i][:].rearrange("p (t m j) -> p m t j", t=PACK, j=PACK)[:, m0:m1]
             s = raw[i][:].rearrange("p j (m t) -> p m t j", t=PACK)[:, m0:m1]
             if eng == "v":
@@ -89,64 +87,42 @@ def tile_picked_zmodd_relu_po_kernel(tc, x_words, x_scales, w0, w1, w2, offs, ce
             for q in range(4):
                 eng.dma_start(out=gs[32 * q : 32 * q + 4, :].bitcast(I32), in_=gs0[32 * q : 32 * q + 32 : 8, :].bitcast(I32))
 
-        def gscales4():
-            nc.vector.tensor_copy(gs[:], xs[:].indirect(offs_t[:]))
-
         def gwords(h):
             nc.vector.tensor_copy(gw[h][:], xw[:].indirect(offs_t[:, 32 * h : 32 * h + 32]))
 
-        def product(i, t, h, b, eng="s"):
-            acc = psum.tile([P, HALF], F32, name="bank%d" % b)
+        def product(i, t, h, eng, func=None):
+            acc = psum.tile([P, HALF], F32, name="bank%d" % (len(accs) % BANKS))
+            accs[(i, t, h)] = acc
             cols = slice(P * t, P * t + P)
             nc.tensor.matmul_mx(out=acc[:], lhsT=wc[i][:, cols].bitcast(FP8X4), lhsT_scale=ws[i][:, cols],
                                 rhs=gw[h][:].bitcast(FP8X4), rhs_scale=gs[:, HALF * h : HALF * h + HALF], start=True, stop=True)
             dst = rows[i][t][:, HALF * h : HALF * h + HALF]
             if eng == "v":
                 nc.vector.tensor_copy(out=dst, in_=acc[:])
-            elif i == 0:
+            elif func is None:
                 nc.scalar.copy(out=dst, in_=acc[:])
             else:
-                nc.scalar.activation(out=dst, in_=acc[:], func=ACT.Sigmoid)
+                nc.scalar.activation(out=dst, in_=acc[:], func=func)
 
-        def both(i, t, b):
-            product(i, t, 0, b)
-            product(i, t, 1, b + 1)
+        def gmask(d, t, a=0, b=V):
+            nc.scalar.activation(out=mask[d][t][:, a:b], in_=rows[M0 + d][t][:].indirect(cen_t[:, a // 16 : b // 16]), func=ACT.Sigmoid)
 
-        def gy(d, t):
-            nc.vector.tensor_copy(yg[d][t], rows[0][t][:].indirect(pos_t[d][:]))
-
-        def open_yg(name, items):
-            held = keep.tile([P, len(items), V], F32, name=name, align_bytes=64)
-            for k, (d, t) in enumerate(items):
-                yg[d][t] = held[:, k, :]
-
-        def open_pr0():
-            first = keep.tile([P, PACK, V], F32, name="xw", align_bytes=64)
+        def open_pr0(name):
+            first = keep.tile([P, PACK, V], F32, name=name, align_bytes=64)
             pr[0] = [first[:, t, :] for t in range(PACK)]
 
         def fused(d, t, a=0, b=V):
-            nc.vector.tensor_tensor(pr[d][t][:, a:b], rows[1 + d][t][:].indirect(cen_t[:, a // 16 : b // 16]), yg[d][t][:, a:b], ALU.mult)
+            nc.vector.tensor_tensor(pr[d][t][:, a:b], rows[Y][t][:].indirect(pos_t[d][:, a // 16 : b // 16]), mask[d][t][:, a:b], ALU.mult)
 
-        def pe_add(t, b):
-            bank = psum.tile([P, V], F32, name="bank%d" % b)
-            for c in range(0, V, P):
-                for d in range(2):
-                    nc.tensor.matmul(bank[:, c : c + P], lhsT=pr[d][t][:, c : c + P], rhs=ident[:], is_transpose=True, start=(d == 0), stop=(d == 1))
-            nc.scalar.activation(out=turned[t][:], in_=bank[:], func=ACT.Relu)
+        def addv(t, a=0, b=V):
+            nc.vector.tensor_tensor(res[:, t, a:b], pr[0][t][:, a:b], pr[1][t][:, a:b], ALU.add)
 
-        def pe_back(t, b):
-            bank = psum.tile([P, V], F32, name="bank%d" % b)
-            for c in range(0, V, P):
-                nc.tensor.transpose(bank[:, c : c + P], turned[t][:, c : c + P], ident[:])
-            nc.scalar.copy(out=res[:, t, :], in_=bank[:])
-            nc.sync.dma_start(out=out_rows[:, t, :], in_=res[:, t, :])
-
-        def addv(t, a, b, eng=nc.vector):
-            eng.tensor_tensor(res[:, t, a:b], pr[0][t][:, a:b], pr[1][t][:, a:b], ALU.add)
-
-        def store(t, dst, a, b):
-            nc.scalar.activation(out=dst[:, a:b], in_=res[:, t, a:b], func=ACT.Relu)
-            nc.sync.dma_start(out=out_rows[:, t, a:b], in_=dst[:, a:b])
+        def store(t, eng, a=0, b=V):
+            if eng == "s":
+                nc.scalar.activation(out=fin[t][:, a:b], in_=res[:, t, a:b], func=ACT.Relu)
+            else:
+                nc.vector.tensor_scalar_max(fin[t][:, a:b], res[:, t, a:b], 0.0)
+            nc.sync.dma_start(out=out_rows[:, t, a:b], in_=fin[t][:, a:b])
 
         def weave(a, b, eng):
             o = og[:, a:b, :]
@@ -173,72 +149,79 @@ def tile_picked_zmodd_relu_po_kernel(tc, x_words, x_scales, w0, w1, w2, offs, ce
         nc.vector.memset(warm[:], 0.0)
         nc.vector.memset(gs[:].bitcast(I32), 0)
         nc.scalar.activation(out=warm2[:], in_=warm[:], func=ACT.Sigmoid)
-        make_identity(nc, ident[:])
-        load_w(0, w0)
+        load_w(M0, "rawA")
         nc.sync.dma_start(offs_t[:], offs)
         load_scales(nc.sync)
-        nc.sync.dma_start(pos1_t[:], pos1)
-        load_x()
-        load_w(1, w1)
-        nc.sync.dma_start(pos2_t[:], pos2)
         nc.sync.dma_start(cen_t[:], cen)
-        deal(0, "s")
-        gscales(nc.scalar)
-        quant(0)
+        load_x()
+        nc.sync.dma_start(pos1_t[:], pos1)
+        nc.sync.dma_start(pos2_t[:], pos2)
+        open_grp(M0, "grpA")
+        deal(M0, "s")
+        gscales(nc.sync)
+        load_w(Y, "xs")
+        quant(M0)
+        load_w(M1, "rawA")
         gwords(0)
         gwords(1)
-        load_w(2, w2)
-        product(0, 0, 0, 0)
-        product(0, 1, 0, 1)
-        product(0, 0, 1, 2)
-        product(0, 1, 1, 3)
-        deal(1, "v")
-        open_yg("raw1", [(0, 0)])
-        gy(0, 0)
-        quant(1)
-        open_yg("grp1", [(1, 0), (0, 1), (1, 1), (0, 2), (1, 2)])
-        gy(1, 0)
-        deal(2, "g")
-        quant(2)
-        open_pr0()
-        both(1, 0, 4)
-        both(1, 1, 6)
-        both(0, 2, 0)
-        both(1, 2, 2)
-        both(0, 3, 4)
-        both(1, 3, 6)
-        both(2, 0, 0)
-        both(2, 1, 2)
-        both(2, 2, 4)
-        both(2, 3, 6)
-        gy(0, 1)
-        gy(1, 1)
-        gy(0, 2)
-        gy(1, 2)
+        open_grp(Y, "grpB")
+        deal(Y, "v")
+        product(M0, 0, 0, "s")
+        product(M0, 1, 0, "s")
+        product(M0, 0, 1, "s")
+        product(M0, 1, 1, "s")
+        quant(Y)
+        open_grp(M1, "grpB")
+        deal(M1, "g")
+        gmask(0, 0)
+        product(Y, 0, 0, "v")
+        product(Y, 0, 1, "v")
+        product(M0, 2, 0, "s")
+        product(M0, 2, 1, "s")
+        gmask(0, 1)
+        product(Y, 1, 0, "v")
+        product(Y, 1, 1, "v")
+        product(M0, 3, 0, "s")
+        product(M0, 3, 1, "s")
+        product(Y, 2, 0, "v")
+        product(Y, 2, 1, "v")
+        quant(M1)
+        open_pr0("grpB")
+        gmask(0, 2)
+        gmask(0, 3)
+        product(Y, 3, 0, "v")
+        product(Y, 3, 1, "v")
         fused(0, 0)
+        product(M1, 0, 0, "s")
+        product(M1, 0, 1, "s")
+        product(M1, 1, 0, "s")
+        gmask(1, 0)
         fused(0, 1)
+        product(M1, 1, 1, "s")
+        product(M1, 2, 0, "s")
+        gmask(1, 1)
         fused(0, 2)
+        product(M1, 2, 1, "s")
+        product(M1, 3, 0, "s")
+        gmask(1, 2)
+        fused(0, 3)
+        product(M1, 3, 1, "s")
         fused(1, 0)
         fused(1, 1)
+        addv(0)
+        gmask(1, 3)
+        addv(1)
+        store(0, "s")
         fused(1, 2)
-        open_yg("rows2_2", [(0, 3), (1, 3)])
-        gy(0, 3)
-        gy(1, 3)
-        pe_add(0, 0)
-        pe_add(1, 1)
-        pe_back(0, 2)
-        pe_add(2, 3)
-        pe_back(1, 4)
-        pe_back(2, 5)
-        fused(0, 3)
+        store(1, "s")
         fused(1, 3, 0, 256)
+        addv(2)
         fused(1, 3, 256, 512)
+        store(2, "s")
         addv(3, 0, 256)
-        last = keep.tile([P, V], F32, name="turned2")
-        store(3, last, 0, 256)
-        weave(0, 192, "s")
         addv(3, 256, 512)
-        store(3, last, 256, 512)
+        weave(0, 192, "s")
+        store(3, "v")
         weave(192, 512, "v")
         quantc(256, 512)
         quantc(0, 256)

@@ -43,9 +43,10 @@ def tile_picked_zmodd_relu_po_kernel(tc, x_words, x_scales, w0, w1, w2, offs, ce
         gs0 = keep.tile([P, S], U8, name="gs0", align_bytes=64)
         gs = keep.tile([P, S], U8, name="gs", align_bytes=64)
         gw = [keep.tile([P, HALF], U32, name="gw%d" % h, align_bytes=64) for h in range(2)]
-        rows = [[keep.tile([P, S], F32, name="rows%d_%d" % (i, t), align_bytes=64) for t in range(PACK)] for i in range(3)]
-        mask = [[keep.tile([P, V], F32, name="mask%d_%d" % (d, t), align_bytes=64) for t in range(PACK)] for d in range(2)]
-        pr = [[None] * PACK, [keep.tile([P, V], F32, name="pr1_%d" % t)[:] for t in range(PACK)]]
+        rows = [[None] * PACK for i in range(3)]
+        mask = [[None] * PACK for d in range(2)]
+        reuse = {}
+        pr = [[None] * PACK for d in range(2)]
         res = keep.tile([P, PACK, V], F32, name="res")
         fin = [keep.tile([P, V], F32, name="fin%d" % t) for t in range(PACK)]
         og = keep.tile([P, V, PACK], BF16, name="og", align_bytes=64)
@@ -56,12 +57,18 @@ def tile_picked_zmodd_relu_po_kernel(tc, x_words, x_scales, w0, w1, w2, offs, ce
         weights = (w0, w1, w2)
         accs = {}
 
+        def hold(old, new):
+            reuse[new] = reuse.get(old, old)
+
+        def fresh(name, width):
+            return keep.tile([P, width], F32, name=reuse.get(name, name), align_bytes=64)
+
         def load_w(i, name):
             raw[i] = keep.tile([P, PACK, N], F32, name=name, align_bytes=64)
             nc.sync.dma_start(out=raw[i][:], in_=weights[i].rearrange("(p j) c -> p j c", j=PACK))
 
         def load_scales(eng):
-            eng.dma_start(out=xs[0:P:8, :].bitcast(I32), in_=x_scales[0].bitcast(I32))
+            eng.dma_start(out=xs[16:32, :].bitcast(I32), in_=x_scales[0].bitcast(I32))
 
         def load_x():
             nc.sync.dma_start(out=xw[:].bitcast(I32), in_=x_words[0].rearrange("p n t -> p (n t)").bitcast(I32))
@@ -85,17 +92,20 @@ def tile_picked_zmodd_relu_po_kernel(tc, x_words, x_scales, w0, w1, w2, offs, ce
         def gscales(eng):
             nc.vector.tensor_copy(gs0[:], xs[:].indirect(offs_t[:]))
             for q in range(4):
-                eng.dma_start(out=gs[32 * q : 32 * q + 4, :].bitcast(I32), in_=gs0[32 * q : 32 * q + 32 : 8, :].bitcast(I32))
+                eng.dma_start(out=gs[32 * q : 32 * q + 4, :].bitcast(I32), in_=gs0[16 + 4 * q : 20 + 4 * q, :].bitcast(I32))
 
         def gwords(h):
             nc.vector.tensor_copy(gw[h][:], xw[:].indirect(offs_t[:, 32 * h : 32 * h + 32]))
 
         def product(i, t, h, eng, func=None):
-            acc = psum.tile([P, HALF], F32, name="bank%d" % (len(accs) % BANKS))
-            accs[(i, t, h)] = acc
+            turn = accs.get(eng, 0)
+            accs[eng] = turn + 1
+            acc = psum.tile([P, HALF], F32, name="bank_%s%d" % (eng, turn % (BANKS // 2)))
             cols = slice(P * t, P * t + P)
             nc.tensor.matmul_mx(out=acc[:], lhsT=wc[i][:, cols].bitcast(FP8X4), lhsT_scale=ws[i][:, cols],
                                 rhs=gw[h][:].bitcast(FP8X4), rhs_scale=gs[:, HALF * h : HALF * h + HALF], start=True, stop=True)
+            if rows[i][t] is None:
+                rows[i][t] = fresh("rows%d_%d" % (i, t), S)
             dst = rows[i][t][:, HALF * h : HALF * h + HALF]
             if eng == "v":
                 nc.vector.tensor_copy(out=dst, in_=acc[:])
@@ -105,13 +115,13 @@ def tile_picked_zmodd_relu_po_kernel(tc, x_words, x_scales, w0, w1, w2, offs, ce
                 nc.scalar.activation(out=dst, in_=acc[:], func=func)
 
         def gmask(d, t, a=0, b=V):
+            if mask[d][t] is None:
+                mask[d][t] = fresh("mask%d_%d" % (d, t), V)
             nc.scalar.activation(out=mask[d][t][:, a:b], in_=rows[M0 + d][t][:].indirect(cen_t[:, a // 16 : b // 16]), func=ACT.Sigmoid)
 
-        def open_pr0(name):
-            first = keep.tile([P, PACK, V], F32, name=name, align_bytes=64)
-            pr[0] = [first[:, t, :] for t in range(PACK)]
-
         def fused(d, t, a=0, b=V):
+            if pr[d][t] is None:
+                pr[d][t] = fresh("pr%d_%d" % (d, t), V)
             nc.vector.tensor_tensor(pr[d][t][:, a:b], rows[Y][t][:].indirect(pos_t[d][:, a // 16 : b // 16]), mask[d][t][:, a:b], ALU.mult)
 
         def addv(t, a=0, b=V):
@@ -145,13 +155,15 @@ def tile_picked_zmodd_relu_po_kernel(tc, x_words, x_scales, w0, w1, w2, offs, ce
             c = keep.tile([P, 1], dt, name=name)
             nc.gpsimd.tensor_copy(c[:], ap)
 
-        nc.vector.memset(xs[:].bitcast(I32), 0)
+        nc.gpsimd.memset(xs[32:64, :].bitcast(I32), 0)
+        nc.vector.memset(xs[0:16, :].bitcast(I32), 0)
+        nc.vector.memset(xs[64:P, :].bitcast(I32), 0)
         nc.vector.memset(warm[:], 0.0)
         nc.vector.memset(gs[:].bitcast(I32), 0)
         nc.scalar.activation(out=warm2[:], in_=warm[:], func=ACT.Sigmoid)
-        load_w(M0, "rawA")
-        nc.sync.dma_start(offs_t[:], offs)
         load_scales(nc.sync)
+        nc.sync.dma_start(offs_t[:], offs)
+        load_w(M0, "rawA")
         nc.sync.dma_start(cen_t[:], cen)
         load_x()
         nc.sync.dma_start(pos1_t[:], pos1)
@@ -166,56 +178,59 @@ def tile_picked_zmodd_relu_po_kernel(tc, x_words, x_scales, w0, w1, w2, offs, ce
         gwords(1)
         open_grp(Y, "grpB")
         deal(Y, "v")
+        hold("xs", "rows1_2")
         product(M0, 0, 0, "s")
         product(M0, 1, 0, "s")
         product(M0, 0, 1, "s")
         product(M0, 1, 1, "s")
         quant(Y)
+        product(M0, 2, 0, "v")
         open_grp(M1, "grpB")
         deal(M1, "g")
         gmask(0, 0)
-        product(Y, 0, 0, "v")
-        product(Y, 0, 1, "v")
-        product(M0, 2, 0, "s")
-        product(M0, 2, 1, "s")
+        product(M0, 2, 1, "v")
         gmask(0, 1)
-        product(Y, 1, 0, "v")
-        product(Y, 1, 1, "v")
+        product(Y, 0, 0, "v")
         product(M0, 3, 0, "s")
+        product(Y, 0, 1, "v")
         product(M0, 3, 1, "s")
-        product(Y, 2, 0, "v")
-        product(Y, 2, 1, "v")
+        product(Y, 1, 0, "v")
         quant(M1)
-        open_pr0("grpB")
+        hold("grpB", "pr0_0")
         gmask(0, 2)
-        gmask(0, 3)
-        product(Y, 3, 0, "v")
-        product(Y, 3, 1, "v")
-        fused(0, 0)
+        product(Y, 1, 1, "v")
         product(M1, 0, 0, "s")
         product(M1, 0, 1, "s")
+        fused(0, 0)
+        product(Y, 2, 0, "v")
         product(M1, 1, 0, "s")
+        product(Y, 2, 1, "v")
         gmask(1, 0)
+        hold("rows2_0", "mask0_3")
         fused(0, 1)
         product(M1, 1, 1, "s")
-        product(M1, 2, 0, "s")
-        gmask(1, 1)
+        gmask(0, 3)
+        fused(1, 0)
         fused(0, 2)
+        gmask(1, 1)
+        addv(0)
+        product(Y, 3, 0, "v")
+        product(Y, 3, 1, "s")
+        product(M1, 2, 0, "s")
         product(M1, 2, 1, "s")
+        fused(1, 1)
+        fused(0, 3)
         product(M1, 3, 0, "s")
         gmask(1, 2)
-        fused(0, 3)
-        product(M1, 3, 1, "s")
-        fused(1, 0)
-        fused(1, 1)
-        addv(0)
-        gmask(1, 3)
         addv(1)
-        store(0, "s")
+        product(M1, 3, 1, "s")
         fused(1, 2)
-        store(1, "s")
-        fused(1, 3, 0, 256)
+        store(0, "s")
+        gmask(1, 3, 0, 256)
+        gmask(1, 3, 256, 512)
         addv(2)
+        fused(1, 3, 0, 256)
+        store(1, "s")
         fused(1, 3, 256, 512)
         store(2, "s")
         addv(3, 0, 256)

@@ -48,7 +48,7 @@ def tile_picked_zmodd_relu_po_kernel(tc, x_words, x_scales, w0, w1, w2, offs, ce
         reuse = {}
         pr = [[None] * PACK for d in range(2)]
         res = keep.tile([P, PACK, V], F32, name="res")
-        fin = [keep.tile([P, V], F32, name="fin%d" % t) for t in range(PACK)]
+        fin = [None] * PACK
         og = keep.tile([P, V, PACK], BF16, name="og", align_bytes=64)
         oc = keep.tile([P, V], U32, name="oc", align_bytes=64)
         osc = keep.tile([P, V], U8, name="osc", align_bytes=64)
@@ -128,6 +128,8 @@ def tile_picked_zmodd_relu_po_kernel(tc, x_words, x_scales, w0, w1, w2, offs, ce
             nc.vector.tensor_tensor(res[:, t, a:b], pr[0][t][:, a:b], pr[1][t][:, a:b], ALU.add)
 
         def store(t, eng, a=0, b=V):
+            if fin[t] is None:
+                fin[t] = fresh("fin%d" % t, V)
             if eng == "s":
                 nc.scalar.activation(out=fin[t][:, a:b], in_=res[:, t, a:b], func=ACT.Relu)
             else:
@@ -206,25 +208,28 @@ def tile_picked_zmodd_relu_po_kernel(tc, x_words, x_scales, w0, w1, w2, offs, ce
         product(M1, 1, 0, "s")
         product(Y, 2, 1, "v")
         gmask(1, 0)
-        hold("rows2_0", "mask0_3")
+        hold("rows2_0", "pr0_2")
         fused(0, 1)
         product(M1, 1, 1, "s")
-        gmask(0, 3)
+        product(M1, 2, 0, "s")
         fused(1, 0)
         fused(0, 2)
         gmask(1, 1)
+        hold("rows2_1", "rows0_3")
         addv(0)
-        product(Y, 3, 0, "v")
-        product(Y, 3, 1, "s")
-        product(M1, 2, 0, "s")
         product(M1, 2, 1, "s")
         fused(1, 1)
-        fused(0, 3)
-        product(M1, 3, 0, "s")
+        product(Y, 3, 0, "v")
+        product(Y, 3, 1, "s")
         gmask(1, 2)
+        hold("rows2_2", "pr0_3")
+        hold("mask1_1", "mask0_3")
+        gmask(0, 3)
         addv(1)
+        product(M1, 3, 0, "s")
         product(M1, 3, 1, "s")
         fused(1, 2)
+        fused(0, 3)
         store(0, "s")
         gmask(1, 3, 0, 256)
         gmask(1, 3, 256, 512)
@@ -235,9 +240,9 @@ def tile_picked_zmodd_relu_po_kernel(tc, x_words, x_scales, w0, w1, w2, offs, ce
         store(2, "s")
         addv(3, 0, 256)
         addv(3, 256, 512)
-        weave(0, 192, "s")
-        store(3, "v")
-        weave(192, 512, "v")
-        quantc(256, 512)
+        weave(0, 256, "v")
+        store(3, "s")
+        weave(256, 512, "v")
         quantc(0, 256)
+        quantc(256, 512)
         scales_out()

@@ -137,8 +137,8 @@ def tile_picked_zmodd_relu_po_kernel(tc, x_words, x_scales, w0, w1, w2, offs, ce
             nc.sync.dma_start(out=out_rows[:, t, a:b], in_=fin[t][:, a:b])
 
         def weave(a, b, eng):
-            o = og[:, a:b, :]
-            s = res[:, :, a:b].rearrange("p t c -> p c t")
+            o = og[:, a:b, :].rearrange("p (c i) t -> p c t i", i=PACK)
+            s = res[:, :, a:b].rearrange("p t (c i) -> p c t i", i=PACK)
             if eng == "s":
                 nc.scalar.activation(out=o, in_=s, func=ACT.Relu)
             else:
@@ -171,9 +171,9 @@ def tile_picked_zmodd_relu_po_kernel(tc, x_words, x_scales, w0, w1, w2, offs, ce
         nc.sync.dma_start(pos1_t[:], pos1)
         nc.sync.dma_start(pos2_t[:], pos2)
         open_grp(M0, "grpA")
-        deal(M0, "s")
         gscales(nc.sync)
         load_w(Y, "xs")
+        deal(M0, "v")
         quant(M0)
         load_w(M1, "rawA")
         gwords(0)

@@ -77,8 +77,9 @@ def tile_picked_zmodd_relu_po_kernel(tc, x_words, x_scales, w0, w1, w2, offs, ce
             grp[i] = keep.tile([P, PACK * N], BF16, name=name, align_bytes=64)
 
         def deal(i, eng, m0=0, m1=P):
-            o = grp[i][:].rearrange("p (t m j) -> p m t j", t=PACK, j=PACK)[:, m0:m1]
-            s = raw[i][:].rearrange("p j (m t) -> p m t j", t=PACK)[:, m0:m1]
+            walk = "p m j t" if eng == "v" else "p m t j"
+            o = grp[i][:].rearrange("p (t m j) -> " + walk, t=PACK, j=PACK)[:, m0:m1]
+            s = raw[i][:].rearrange("p j (m t) -> " + walk, t=PACK)[:, m0:m1]
             if eng == "v":
                 nc.vector.tensor_copy(out=o, in_=s)
             elif eng == "g":

@@ -26,6 +26,7 @@ def tile_picked_zmodd_relu_po_kernel(tc, x_words, x_scales, w0, w1, w2, offs, ce
     nc = tc.nc
     with ExitStack() as ctx:
         keep = ctx.enter_context(tc.tile_pool(name="keep", bufs=1))
+        shared = ctx.enter_context(tc.tile_pool(name="shared", bufs=1))
         psum = ctx.enter_context(tc.psum_pool(name="psum", bufs=1))
 
         offs_t = keep.tile([P, S // 16], U16, name="offs_t")
@@ -33,8 +34,8 @@ def tile_picked_zmodd_relu_po_kernel(tc, x_words, x_scales, w0, w1, w2, offs, ce
         pos1_t = keep.tile([P, V // 16], U16, name="pos1_t")
         pos2_t = keep.tile([P, V // 16], U16, name="pos2_t")
         xw = keep.tile([P, T], U32, name="xw", align_bytes=64)
-        xs = keep.tile([P, T], U8, name="xs", align_bytes=64)
-        raw = [None] * 3
+        xs = shared.tile([P, T], U8, name="xs", align_bytes=64, offset=T // 2)
+        raw = [[None] * 2 for i in range(3)]
         grp = [None] * 3
         wc = [keep.tile([P, N], U32, name="wc%d" % i, align_bytes=64) for i in range(3)]
         ws = [keep.tile([P, N], U8, name="ws%d" % i, align_bytes=64) for i in range(3)]
@@ -46,6 +47,7 @@ def tile_picked_zmodd_relu_po_kernel(tc, x_words, x_scales, w0, w1, w2, offs, ce
         rows = [[None] * PACK for i in range(3)]
         mask = [[None] * PACK for d in range(2)]
         reuse = {}
+        placed = {"rows1_2": T // 2, "rows1_3": 3 * T // 2, "grp0": 3 * T, "grp2": 3 * T, "pr0_0": 3 * T - 1024, "pr0_1": 3 * T + 1024, "pr0_2": 3 * T + 3072}
         pr = [[None] * PACK for d in range(2)]
         res = keep.tile([P, PACK, V], F32, name="res")
         fin = [None] * PACK
@@ -60,12 +62,17 @@ def tile_picked_zmodd_relu_po_kernel(tc, x_words, x_scales, w0, w1, w2, offs, ce
         def hold(old, new):
             reuse[new] = reuse.get(old, old)
 
-        def fresh(name, width):
-            return keep.tile([P, width], F32, name=reuse.get(name, name), align_bytes=64)
+        def fresh(name, width, dt=F32):
+            if name in placed:
+                return shared.tile([P, width], dt, name=name, align_bytes=64, offset=placed[name])
+            return keep.tile([P, width], dt, name=reuse.get(name, name), align_bytes=64)
 
-        def load_w(i, name):
-            raw[i] = keep.tile([P, PACK, N], F32, name=name, align_bytes=64)
-            nc.sync.dma_start(out=raw[i][:], in_=weights[i].rearrange("(p j) c -> p j c", j=PACK))
+        def load_w(i, h, name):
+            if name is None:
+                raw[i][h] = shared.tile([P, PACK, N // 2], F32, name="rawY%d" % h, align_bytes=64, offset=T * h)
+            else:
+                raw[i][h] = keep.tile([P, PACK, N // 2], F32, name=name, align_bytes=64)
+            nc.sync.dma_start(out=raw[i][h][:], in_=weights[i].rearrange("(p j) c -> p j c", j=PACK)[:, :, N // 2 * h : N // 2 * (h + 1)])
 
         def load_scales(eng):
             eng.dma_start(out=xs[16:32, :].bitcast(I32), in_=x_scales[0].bitcast(I32))
@@ -73,13 +80,12 @@ def tile_picked_zmodd_relu_po_kernel(tc, x_words, x_scales, w0, w1, w2, offs, ce
         def load_x():
             nc.sync.dma_start(out=xw[:].bitcast(I32), in_=x_words[0].rearrange("p n t -> p (n t)").bitcast(I32))
 
-        def open_grp(i, name):
-            grp[i] = keep.tile([P, PACK * N], BF16, name=name, align_bytes=64)
-
-        def deal(i, eng, m0=0, m1=P):
+        def deal(i, h, t0, t1, eng):
+            if grp[i] is None:
+                grp[i] = fresh("grp%d" % i, PACK * N, BF16)
             walk = "p m j t" if eng == "v" else "p m t j"
-            o = grp[i][:].rearrange("p (t m j) -> " + walk, t=PACK, j=PACK)[:, m0:m1]
-            s = raw[i][:].rearrange("p j (m t) -> " + walk, t=PACK)[:, m0:m1]
+            o = grp[i][:].rearrange("p (t m j) -> p t m j", t=PACK, j=PACK)[:, t0:t1, P // 2 * h : P // 2 * (h + 1), :].rearrange("p t m j -> " + walk)
+            s = raw[i][h][:].rearrange("p j (m t) -> p j m t", t=PACK)[:, :, :, t0:t1].rearrange("p j m t -> " + walk)
             if eng == "v":
                 nc.vector.tensor_copy(out=o, in_=s)
             elif eng == "g":
@@ -87,7 +93,7 @@ def tile_picked_zmodd_relu_po_kernel(tc, x_words, x_scales, w0, w1, w2, offs, ce
             else:
                 nc.scalar.copy(out=o, in_=s)
 
-        def quant(i, t0=0, t1=PACK):
+        def quant(i, t0, t1):
             nc.vector.quantize_mx(out=wc[i][:, P * t0 : P * t1].bitcast(FP8X4), scales=ws[i][:, P * t0 : P * t1], in_=grp[i][:, N * t0 : N * t1])
 
         def gscales(eng):
@@ -154,10 +160,6 @@ def tile_picked_zmodd_relu_po_kernel(tc, x_words, x_scales, w0, w1, w2, offs, ce
                 eng = nc.scalar if q % 2 == 0 else nc.sync
                 eng.dma_start(out=out_2[0, 4 * q : 4 * q + 4, :].bitcast(I32), in_=osc[32 * q : 32 * q + 4, :].bitcast(I32))
 
-        def clock(name, ap, dt):
-            c = keep.tile([P, 1], dt, name=name)
-            nc.gpsimd.tensor_copy(c[:], ap)
-
         nc.gpsimd.memset(xs[32:64, :].bitcast(I32), 0)
         nc.vector.memset(xs[0:16, :].bitcast(I32), 0)
         nc.vector.memset(xs[64:P, :].bitcast(I32), 0)
@@ -166,74 +168,79 @@ def tile_picked_zmodd_relu_po_kernel(tc, x_words, x_scales, w0, w1, w2, offs, ce
         nc.scalar.activation(out=warm2[:], in_=warm[:], func=ACT.Sigmoid)
         load_scales(nc.sync)
         nc.sync.dma_start(offs_t[:], offs)
-        load_w(M0, "rawA")
         nc.sync.dma_start(cen_t[:], cen)
-        load_x()
         nc.sync.dma_start(pos1_t[:], pos1)
+        load_x()
+        load_w(M0, 0, "rawA0")
+        load_w(M0, 1, "rawA1")
         nc.sync.dma_start(pos2_t[:], pos2)
-        open_grp(M0, "grpA")
         gscales(nc.sync)
-        load_w(Y, "xs")
-        deal(M0, "v")
-        quant(M0)
-        load_w(M1, "rawA")
+        load_w(Y, 0, None)
+        load_w(Y, 1, None)
         gwords(0)
         gwords(1)
-        open_grp(Y, "grpB")
-        deal(Y, "v")
-        hold("xs", "rows1_2")
+        deal(M0, 0, 0, 4, "s")
+        load_w(M1, 0, "xw")
+        load_w(M1, 1, "rawA0")
+        deal(M0, 1, 0, 2, "v")
+        deal(M0, 1, 2, 4, "s")
+        quant(M0, 0, 1)
+        quant(M0, 1, 2)
+        quant(M0, 2, 4)
         product(M0, 0, 0, "s")
-        product(M0, 1, 0, "s")
         product(M0, 0, 1, "s")
+        deal(Y, 0, 0, 4, "v")
+        product(M0, 1, 0, "s")
         product(M0, 1, 1, "s")
-        quant(Y)
-        product(M0, 2, 0, "v")
-        open_grp(M1, "grpB")
-        deal(M1, "g")
+        deal(Y, 1, 0, 2, "v")
+        deal(Y, 1, 2, 4, "v")
+        quant(Y, 0, 2)
+        quant(Y, 2, 4)
+        deal(M1, 0, 0, 4, "g")
+        deal(M1, 1, 0, 4, "g")
         gmask(0, 0)
+        product(M0, 2, 0, "v")
         product(M0, 2, 1, "v")
         gmask(0, 1)
-        product(Y, 0, 0, "v")
-        product(M0, 3, 0, "s")
-        product(Y, 0, 1, "v")
-        product(M0, 3, 1, "s")
-        product(Y, 1, 0, "v")
-        quant(M1)
-        hold("grpB", "pr0_0")
+        product(M0, 3, 0, "v")
+        product(M0, 3, 1, "v")
         gmask(0, 2)
-        product(Y, 1, 1, "v")
+        product(Y, 0, 0, "v")
+        product(Y, 0, 1, "v")
+        product(Y, 1, 0, "s")
+        product(Y, 1, 1, "s")
+        quant(M1, 0, 2)
+        quant(M1, 2, 4)
         product(M1, 0, 0, "s")
         product(M1, 0, 1, "s")
         fused(0, 0)
+        gmask(0, 3)
         product(Y, 2, 0, "v")
-        product(M1, 1, 0, "s")
         product(Y, 2, 1, "v")
         gmask(1, 0)
-        hold("rows2_0", "pr0_2")
         fused(0, 1)
+        product(M1, 1, 0, "s")
         product(M1, 1, 1, "s")
-        product(M1, 2, 0, "s")
-        fused(1, 0)
         fused(0, 2)
+        hold("rows2_0", "rows0_3")
+        product(Y, 3, 0, "s")
+        fused(1, 0)
         gmask(1, 1)
-        hold("rows2_1", "rows0_3")
-        addv(0)
+        product(Y, 3, 1, "v")
+        product(M1, 2, 0, "s")
         product(M1, 2, 1, "s")
+        addv(0)
         fused(1, 1)
-        product(Y, 3, 0, "v")
-        product(Y, 3, 1, "s")
-        gmask(1, 2)
-        hold("rows2_2", "pr0_3")
-        hold("mask1_1", "mask0_3")
-        gmask(0, 3)
-        addv(1)
         product(M1, 3, 0, "s")
+        fused(0, 3)
+        gmask(1, 2)
+        addv(1)
         product(M1, 3, 1, "s")
         fused(1, 2)
-        fused(0, 3)
-        store(0, "s")
         gmask(1, 3, 0, 256)
         gmask(1, 3, 256, 512)
+        hold("rows2_3", "fin0")
+        store(0, "s")
         addv(2)
         fused(1, 3, 0, 256)
         store(1, "s")

@@ -47,9 +47,11 @@ def tile_picked_zmodd_relu_po_kernel(tc, x_words, x_scales, w0, w1, w2, offs, ce
         rows = [[None] * PACK for i in range(3)]
         mask = [[None] * PACK for d in range(2)]
         reuse = {}
-        placed = {"rows1_2": T // 2, "rows1_3": 3 * T // 2, "grp0": 3 * T, "grp2": 3 * T, "pr0_0": 3 * T - 1024, "pr0_1": 3 * T + 1024, "pr0_2": 3 * T + 3072}
+        placed = {"raw0_0": 0, "raw0_1": T, "rows1_2": T // 2, "rows1_3": 3 * T // 2,
+                  "grp0": 3 * T, "grp2": 3 * T, "pr0_0": 3 * T - 1024, "pr0_1": 3 * T + 1024, "pr0_2": 3 * T + 3072,
+                  "rows2_2": 6 * T, "fin0": 6 * T - 1024, "fin1": 6 * T + 1024, "fin2": 6 * T + 3072,
+                  "raw1_0": 12 * T, "raw2_1": 12 * T}
         pr = [[None] * PACK for d in range(2)]
-        res = keep.tile([P, PACK, V], F32, name="res")
         fin = [None] * PACK
         og = keep.tile([P, V, PACK], BF16, name="og", align_bytes=64)
         oc = keep.tile([P, V], U32, name="oc", align_bytes=64)
@@ -58,6 +60,7 @@ def tile_picked_zmodd_relu_po_kernel(tc, x_words, x_scales, w0, w1, w2, offs, ce
         pos_t = (pos1_t, pos2_t)
         weights = (w0, w1, w2)
         accs = {}
+        sums = []
 
         def hold(old, new):
             reuse[new] = reuse.get(old, old)
@@ -67,12 +70,9 @@ def tile_picked_zmodd_relu_po_kernel(tc, x_words, x_scales, w0, w1, w2, offs, ce
                 return shared.tile([P, width], dt, name=name, align_bytes=64, offset=placed[name])
             return keep.tile([P, width], dt, name=reuse.get(name, name), align_bytes=64)
 
-        def load_w(i, h, name):
-            if name is None:
-                raw[i][h] = shared.tile([P, PACK, N // 2], F32, name="rawY%d" % h, align_bytes=64, offset=T * h)
-            else:
-                raw[i][h] = keep.tile([P, PACK, N // 2], F32, name=name, align_bytes=64)
-            nc.sync.dma_start(out=raw[i][h][:], in_=weights[i].rearrange("(p j) c -> p j c", j=PACK)[:, :, N // 2 * h : N // 2 * (h + 1)])
+        def load_w(i, h):
+            raw[i][h] = fresh("raw%d_%d" % (i, h), PACK * N // 2)[:].rearrange("p (j c) -> p j c", j=PACK)
+            nc.sync.dma_start(out=raw[i][h], in_=weights[i].rearrange("(p j) c -> p j c", j=PACK)[:, :, N // 2 * h : N // 2 * (h + 1)])
 
         def load_scales(eng):
             eng.dma_start(out=xs[16:32, :].bitcast(I32), in_=x_scales[0].bitcast(I32))
@@ -85,7 +85,7 @@ def tile_picked_zmodd_relu_po_kernel(tc, x_words, x_scales, w0, w1, w2, offs, ce
                 grp[i] = fresh("grp%d" % i, PACK * N, BF16)
             walk = "p m j t" if eng == "v" else "p m t j"
             o = grp[i][:].rearrange("p (t m j) -> p t m j", t=PACK, j=PACK)[:, t0:t1, P // 2 * h : P // 2 * (h + 1), :].rearrange("p t m j -> " + walk)
-            s = raw[i][h][:].rearrange("p j (m t) -> p j m t", t=PACK)[:, :, :, t0:t1].rearrange("p j m t -> " + walk)
+            s = raw[i][h].rearrange("p j (m t) -> p j m t", t=PACK)[:, :, :, t0:t1].rearrange("p j m t -> " + walk)
             if eng == "v":
                 nc.vector.tensor_copy(out=o, in_=s)
             elif eng == "g":
@@ -132,20 +132,23 @@ def tile_picked_zmodd_relu_po_kernel(tc, x_words, x_scales, w0, w1, w2, offs, ce
             nc.vector.tensor_tensor(pr[d][t][:, a:b], rows[Y][t][:].indirect(pos_t[d][:, a // 16 : b // 16]), mask[d][t][:, a:b], ALU.mult)
 
         def addv(t, a=0, b=V):
-            nc.vector.tensor_tensor(res[:, t, a:b], pr[0][t][:, a:b], pr[1][t][:, a:b], ALU.add)
+            if not sums:
+                sums.append(fresh("res", PACK * V)[:].rearrange("p (t c) -> p t c", t=PACK))
+            nc.vector.tensor_tensor(sums[0][:, t, a:b], pr[0][t][:, a:b], pr[1][t][:, a:b], ALU.add)
 
         def store(t, eng, a=0, b=V):
             if fin[t] is None:
                 fin[t] = fresh("fin%d" % t, V)
             if eng == "s":
-                nc.scalar.activation(out=fin[t][:, a:b], in_=res[:, t, a:b], func=ACT.Relu)
+                nc.scalar.activation(out=fin[t][:, a:b], in_=sums[0][:, t, a:b], func=ACT.Relu)
             else:
-                nc.vector.tensor_scalar_max(fin[t][:, a:b], res[:, t, a:b], 0.0)
-            nc.sync.dma_start(out=out_rows[:, t, a:b], in_=fin[t][:, a:b])
+                nc.vector.tensor_scalar_max(fin[t][:, a:b], sums[0][:, t, a:b], 0.0)
+            if b == V:
+                nc.sync.dma_start(out=out_rows[:, t, :], in_=fin[t][:])
 
         def weave(a, b, eng):
             o = og[:, a:b, :].rearrange("p (c i) t -> p c t i", i=PACK)
-            s = res[:, :, a:b].rearrange("p t (c i) -> p c t i", i=PACK)
+            s = sums[0][:, :, a:b].rearrange("p t (c i) -> p c t i", i=PACK)
             if eng == "s":
                 nc.scalar.activation(out=o, in_=s, func=ACT.Relu)
             else:
@@ -171,17 +174,18 @@ def tile_picked_zmodd_relu_po_kernel(tc, x_words, x_scales, w0, w1, w2, offs, ce
         nc.sync.dma_start(cen_t[:], cen)
         nc.sync.dma_start(pos1_t[:], pos1)
         load_x()
-        load_w(M0, 0, "rawA0")
-        load_w(M0, 1, "rawA1")
+        load_w(M0, 0)
+        load_w(M0, 1)
         nc.sync.dma_start(pos2_t[:], pos2)
         gscales(nc.sync)
-        load_w(Y, 0, None)
-        load_w(Y, 1, None)
+        load_w(Y, 0)
+        load_w(Y, 1)
         gwords(0)
         gwords(1)
         deal(M0, 0, 0, 4, "s")
-        load_w(M1, 0, "xw")
-        load_w(M1, 1, "rawA0")
+        hold("xw", "raw2_0")
+        load_w(M1, 0)
+        load_w(M1, 1)
         deal(M0, 1, 0, 2, "v")
         deal(M0, 1, 2, 4, "s")
         quant(M0, 0, 1)
@@ -237,19 +241,19 @@ def tile_picked_zmodd_relu_po_kernel(tc, x_words, x_scales, w0, w1, w2, offs, ce
         addv(1)
         product(M1, 3, 1, "s")
         fused(1, 2)
+        store(0, "s")
         gmask(1, 3, 0, 256)
         gmask(1, 3, 256, 512)
-        hold("rows2_3", "fin0")
-        store(0, "s")
+        store(1, "v")
         addv(2)
         fused(1, 3, 0, 256)
-        store(1, "s")
         fused(1, 3, 256, 512)
         store(2, "s")
         addv(3, 0, 256)
         addv(3, 256, 512)
+        store(3, "s", 0, 256)
+        store(3, "s", 256, 512)
         weave(0, 256, "v")
-        store(3, "s")
         weave(256, 512, "v")
         quantc(0, 256)
         quantc(256, 512)

@@ -20,6 +20,7 @@ PACK = 4
 HALF = 512
 BANKS = 8
 Y, M0, M1 = 0, 1, 2
+PIECES = ((0, 256, 384, 512), (0, 256, 512), (0, 256, 512))
 
 
 def tile_picked_zmodd_relu_po_kernel(tc, x_words, x_scales, w0, w1, w2, offs, cen, pos1, pos2, out_0, out_1, out_2):
@@ -34,8 +35,8 @@ def tile_picked_zmodd_relu_po_kernel(tc, x_words, x_scales, w0, w1, w2, offs, ce
         pos1_t = keep.tile([P, V // 16], U16, name="pos1_t")
         pos2_t = keep.tile([P, V // 16], U16, name="pos2_t")
         xw = keep.tile([P, T], U32, name="xw", align_bytes=64)
-        xs = shared.tile([P, T], U8, name="xs", align_bytes=64, offset=T // 2)
-        raw = [[None] * 2 for i in range(3)]
+        xs = shared.tile([P, T], U8, name="xs", align_bytes=64, offset=T - 64)
+        raw = [[None] * 3 for i in range(3)]
         grp = [None] * 3
         wc = [keep.tile([P, N], U32, name="wc%d" % i, align_bytes=64) for i in range(3)]
         ws = [keep.tile([P, N], U8, name="ws%d" % i, align_bytes=64) for i in range(3)]
@@ -47,7 +48,7 @@ def tile_picked_zmodd_relu_po_kernel(tc, x_words, x_scales, w0, w1, w2, offs, ce
         rows = [[None] * PACK for i in range(3)]
         mask = [[None] * PACK for d in range(2)]
         reuse = {}
-        placed = {"raw0_0": 0, "raw0_1": T, "rows1_2": T // 2, "rows1_3": 3 * T // 2,
+        placed = {"raw0_0": 0, "raw0_1": T, "raw0_2": 3 * T // 2, "rows1_2": 3 * T // 4, "rows1_3": 7 * T // 4,
                   "grp0": 3 * T, "grp2": 3 * T, "pr0_0": 3 * T - 1024, "pr0_1": 3 * T + 1024, "pr0_2": 3 * T + 3072,
                   "rows2_2": 6 * T, "fin0": 6 * T - 1024, "fin1": 6 * T + 1024, "fin2": 6 * T + 3072,
                   "raw1_0": 12 * T, "raw2_1": 12 * T}
@@ -71,8 +72,9 @@ def tile_picked_zmodd_relu_po_kernel(tc, x_words, x_scales, w0, w1, w2, offs, ce
             return keep.tile([P, width], dt, name=reuse.get(name, name), align_bytes=64)
 
         def load_w(i, h):
-            raw[i][h] = fresh("raw%d_%d" % (i, h), PACK * N // 2)[:].rearrange("p (j c) -> p j c", j=PACK)
-            nc.sync.dma_start(out=raw[i][h], in_=weights[i].rearrange("(p j) c -> p j c", j=PACK)[:, :, N // 2 * h : N // 2 * (h + 1)])
+            c0, c1 = PIECES[i][h], PIECES[i][h + 1]
+            raw[i][h] = fresh("raw%d_%d" % (i, h), PACK * (c1 - c0))[:].rearrange("p (j c) -> p j c", j=PACK)
+            nc.sync.dma_start(out=raw[i][h], in_=weights[i].rearrange("(p j) c -> p j c", j=PACK)[:, :, c0:c1])
 
         def load_scales(eng):
             eng.dma_start(out=xs[16:32, :].bitcast(I32), in_=x_scales[0].bitcast(I32))
@@ -84,7 +86,7 @@ def tile_picked_zmodd_relu_po_kernel(tc, x_words, x_scales, w0, w1, w2, offs, ce
             if grp[i] is None:
                 grp[i] = fresh("grp%d" % i, PACK * N, BF16)
             walk = "p m j t" if eng == "v" else "p m t j"
-            o = grp[i][:].rearrange("p (t m j) -> p t m j", t=PACK, j=PACK)[:, t0:t1, P // 2 * h : P // 2 * (h + 1), :].rearrange("p t m j -> " + walk)
+            o = grp[i][:].rearrange("p (t m j) -> p t m j", t=PACK, j=PACK)[:, t0:t1, PIECES[i][h] // PACK : PIECES[i][h + 1] // PACK, :].rearrange("p t m j -> " + walk)
             s = raw[i][h].rearrange("p j (m t) -> p j m t", t=PACK)[:, :, :, t0:t1].rearrange("p j m t -> " + walk)
             if eng == "v":
                 nc.vector.tensor_copy(out=o, in_=s)
@@ -104,22 +106,20 @@ def tile_picked_zmodd_relu_po_kernel(tc, x_words, x_scales, w0, w1, w2, offs, ce
         def gwords(h):
             nc.vector.tensor_copy(gw[h][:], xw[:].indirect(offs_t[:, 32 * h : 32 * h + 32]))
 
-        def product(i, t, h, eng, func=None):
+        def product(i, t, h, eng, a=0, b=HALF):
             turn = accs.get(eng, 0)
             accs[eng] = turn + 1
             acc = psum.tile([P, HALF], F32, name="bank_%s%d" % (eng, turn % (BANKS // 2)))
             cols = slice(P * t, P * t + P)
-            nc.tensor.matmul_mx(out=acc[:], lhsT=wc[i][:, cols].bitcast(FP8X4), lhsT_scale=ws[i][:, cols],
-                                rhs=gw[h][:].bitcast(FP8X4), rhs_scale=gs[:, HALF * h : HALF * h + HALF], start=True, stop=True)
+            nc.tensor.matmul_mx(out=acc[:, 0 : b - a], lhsT=wc[i][:, cols].bitcast(FP8X4), lhsT_scale=ws[i][:, cols],
+                                rhs=gw[h][:, a:b].bitcast(FP8X4), rhs_scale=gs[:, HALF * h + a : HALF * h + b], start=True, stop=True)
             if rows[i][t] is None:
                 rows[i][t] = fresh("rows%d_%d" % (i, t), S)
-            dst = rows[i][t][:, HALF * h : HALF * h + HALF]
+            dst = rows[i][t][:, HALF * h + a : HALF * h + b]
             if eng == "v":
-                nc.vector.tensor_copy(out=dst, in_=acc[:])
-            elif func is None:
-                nc.scalar.copy(out=dst, in_=acc[:])
+                nc.vector.tensor_copy(out=dst, in_=acc[:, 0 : b - a])
             else:
-                nc.scalar.activation(out=dst, in_=acc[:], func=func)
+                nc.scalar.copy(out=dst, in_=acc[:, 0 : b - a])
 
         def gmask(d, t, a=0, b=V):
             if mask[d][t] is None:
@@ -180,6 +180,7 @@ def tile_picked_zmodd_relu_po_kernel(tc, x_words, x_scales, w0, w1, w2, offs, ce
         gscales(nc.sync)
         load_w(Y, 0)
         load_w(Y, 1)
+        load_w(Y, 2)
         gwords(0)
         gwords(1)
         deal(M0, 0, 0, 4, "s")
@@ -196,8 +197,9 @@ def tile_picked_zmodd_relu_po_kernel(tc, x_words, x_scales, w0, w1, w2, offs, ce
         deal(Y, 0, 0, 4, "v")
         product(M0, 1, 0, "s")
         product(M0, 1, 1, "s")
-        deal(Y, 1, 0, 2, "v")
-        deal(Y, 1, 2, 4, "v")
+        deal(Y, 1, 0, 4, "v")
+        deal(Y, 2, 0, 2, "v")
+        deal(Y, 2, 2, 4, "v")
         quant(Y, 0, 2)
         quant(Y, 2, 4)
         deal(M1, 0, 0, 4, "g")
@@ -211,8 +213,9 @@ def tile_picked_zmodd_relu_po_kernel(tc, x_words, x_scales, w0, w1, w2, offs, ce
         gmask(0, 2)
         product(Y, 0, 0, "v")
         product(Y, 0, 1, "v")
+        product(Y, 1, 1, "v", 256, 512)
         product(Y, 1, 0, "s")
-        product(Y, 1, 1, "s")
+        product(Y, 1, 1, "s", 0, 256)
         quant(M1, 0, 2)
         quant(M1, 2, 4)
         product(M1, 0, 0, "s")

@@ -48,10 +48,11 @@ def tile_picked_zmodd_relu_po_kernel(tc, x_words, x_scales, w0, w1, w2, offs, ce
         rows = [[None] * PACK for i in range(3)]
         mask = [[None] * PACK for d in range(2)]
         reuse = {}
-        placed = {"raw0_0": 0, "raw0_1": T, "raw0_2": 3 * T // 2, "rows1_2": 3 * T // 4, "rows1_3": 7 * T // 4,
-                  "grp0": 3 * T, "grp2": 3 * T, "pr0_0": 3 * T - 1024, "pr0_1": 3 * T + 1024, "pr0_2": 3 * T + 3072,
+        placed = {"raw0_0": 0, "raw0_1": T, "raw0_2": 3 * T // 2, "rows1_0": 3 * T // 4,
+                  "grp0": 3 * T, "grp2": 3 * T, "pr0_0": 12 * T - 1024, "pr0_1": 12 * T + 1024, "pr0_2": 12 * T + 3072,
                   "rows2_2": 6 * T, "fin0": 6 * T - 1024, "fin1": 6 * T + 1024, "fin2": 6 * T + 3072,
-                  "raw1_0": 12 * T, "raw2_1": 12 * T}
+                  "raw1_0": 12 * T, "raw2_1": 12 * T,
+                  "rows2_1": 9 * T, "pr0_3": 9 * T}
         pr = [[None] * PACK for d in range(2)]
         fin = [None] * PACK
         og = keep.tile([P, V, PACK], BF16, name="og", align_bytes=64)
@@ -60,7 +61,7 @@ def tile_picked_zmodd_relu_po_kernel(tc, x_words, x_scales, w0, w1, w2, offs, ce
         out_rows = out_0.rearrange("(p t) c -> p t c", t=PACK)
         pos_t = (pos1_t, pos2_t)
         weights = (w0, w1, w2)
-        accs = {}
+        mixed = []
         sums = []
 
         def hold(old, new):
@@ -95,6 +96,28 @@ def tile_picked_zmodd_relu_po_kernel(tc, x_words, x_scales, w0, w1, w2, offs, ce
             else:
                 nc.scalar.copy(out=o, in_=s)
 
+        def deal_mixed(h, eng):
+            if grp[M0] is None:
+                grp[M0] = fresh("grp1", PACK * N, BF16)
+            o = grp[M0][:, N * (2 + h) : N * (3 + h)].rearrange("p (u m j) -> p m u j", u=2, j=PACK)
+            s = raw[M0][h].rearrange("p j (m t) -> p m t j", t=PACK)[:, :, 2:4, :]
+            if eng == "v":
+                nc.vector.tensor_copy(out=o.rearrange("p m u j -> p m j u"), in_=s.rearrange("p m u j -> p m j u"))
+            else:
+                nc.scalar.copy(out=o, in_=s)
+
+        def unmix(step):
+            if step == 0:
+                mask[0][3] = fresh("mask0_3", V)
+                nc.sync.dma_start(out=mask[0][3][0:64, :], in_=mask[0][2][64:P, :])
+            else:
+                nc.sync.dma_start(out=mask[0][3][64:P, :], in_=mixed[0][64:P, :])
+                nc.sync.dma_start(out=mask[0][2][64:P, :], in_=mixed[0][0:64, :])
+
+        def gmixed():
+            mixed.append(fresh("mixed", V))
+            nc.scalar.activation(out=mixed[0][:], in_=rows[M0][3][:].indirect(cen_t[:]), func=ACT.Sigmoid)
+
         def quant(i, t0, t1):
             nc.vector.quantize_mx(out=wc[i][:, P * t0 : P * t1].bitcast(FP8X4), scales=ws[i][:, P * t0 : P * t1], in_=grp[i][:, N * t0 : N * t1])
 
@@ -106,10 +129,8 @@ def tile_picked_zmodd_relu_po_kernel(tc, x_words, x_scales, w0, w1, w2, offs, ce
         def gwords(h):
             nc.vector.tensor_copy(gw[h][:], xw[:].indirect(offs_t[:, 32 * h : 32 * h + 32]))
 
-        def product(i, t, h, eng, a=0, b=HALF):
-            turn = accs.get(eng, 0)
-            accs[eng] = turn + 1
-            acc = psum.tile([P, HALF], F32, name="bank_%s%d" % (eng, turn % (BANKS // 2)))
+        def product(i, t, h, eng, bank, a=0, b=HALF):
+            acc = psum.tile([P, HALF], F32, name="bank%d" % bank)
             cols = slice(P * t, P * t + P)
             nc.tensor.matmul_mx(out=acc[:, 0 : b - a], lhsT=wc[i][:, cols].bitcast(FP8X4), lhsT_scale=ws[i][:, cols],
                                 rhs=gw[h][:, a:b].bitcast(FP8X4), rhs_scale=gs[:, HALF * h + a : HALF * h + b], start=True, stop=True)
@@ -183,20 +204,23 @@ def tile_picked_zmodd_relu_po_kernel(tc, x_words, x_scales, w0, w1, w2, offs, ce
         load_w(Y, 2)
         gwords(0)
         gwords(1)
-        deal(M0, 0, 0, 4, "s")
+        deal_mixed(0, "s")
+        deal(M0, 0, 0, 2, "s")
+        deal_mixed(1, "s")
         hold("xw", "raw2_0")
         load_w(M1, 0)
         load_w(M1, 1)
+        quant(M0, 2, 3)
         deal(M0, 1, 0, 2, "v")
-        deal(M0, 1, 2, 4, "s")
-        quant(M0, 0, 1)
-        quant(M0, 1, 2)
-        quant(M0, 2, 4)
-        product(M0, 0, 0, "s")
-        product(M0, 0, 1, "s")
+        quant(M0, 3, 4)
+        quant(M0, 0, 2)
+        product(M0, 2, 0, "s", 0)
+        product(M0, 2, 1, "s", 1)
+        product(M0, 3, 0, "s", 2)
         deal(Y, 0, 0, 4, "v")
-        product(M0, 1, 0, "s")
-        product(M0, 1, 1, "s")
+        gmask(0, 2)
+        unmix(0)
+        product(M0, 3, 1, "s", 3)
         deal(Y, 1, 0, 4, "v")
         deal(Y, 2, 0, 2, "v")
         deal(Y, 2, 2, 4, "v")
@@ -204,51 +228,50 @@ def tile_picked_zmodd_relu_po_kernel(tc, x_words, x_scales, w0, w1, w2, offs, ce
         quant(Y, 2, 4)
         deal(M1, 0, 0, 4, "g")
         deal(M1, 1, 0, 4, "g")
+        product(M0, 0, 0, "v", 4)
+        product(M0, 0, 1, "v", 5)
+        product(M0, 1, 0, "s", 0)
+        gmixed()
+        unmix(1)
+        product(M0, 1, 1, "s", 1)
         gmask(0, 0)
-        product(M0, 2, 0, "v")
-        product(M0, 2, 1, "v")
         gmask(0, 1)
-        product(M0, 3, 0, "v")
-        product(M0, 3, 1, "v")
-        gmask(0, 2)
-        product(Y, 0, 0, "v")
-        product(Y, 0, 1, "v")
-        product(Y, 1, 1, "v", 256, 512)
-        product(Y, 1, 0, "s")
-        product(Y, 1, 1, "s", 0, 256)
+        product(Y, 0, 0, "v", 6)
+        product(Y, 0, 1, "v", 7)
+        product(Y, 1, 0, "v", 4)
+        product(Y, 1, 1, "v", 5)
+        product(Y, 2, 0, "v", 6)
+        product(Y, 2, 1, "v", 7)
         quant(M1, 0, 2)
         quant(M1, 2, 4)
-        product(M1, 0, 0, "s")
-        product(M1, 0, 1, "s")
+        product(M1, 0, 0, "s", 2)
+        product(M1, 0, 1, "s", 3)
+        product(M1, 1, 0, "s", 0)
         fused(0, 0)
-        gmask(0, 3)
-        product(Y, 2, 0, "v")
-        product(Y, 2, 1, "v")
         gmask(1, 0)
         fused(0, 1)
-        product(M1, 1, 0, "s")
-        product(M1, 1, 1, "s")
         fused(0, 2)
-        hold("rows2_0", "rows0_3")
-        product(Y, 3, 0, "s")
         fused(1, 0)
+        hold("rows2_0", "rows0_3")
+        product(M1, 1, 1, "s", 1)
+        product(Y, 3, 0, "s", 4)
+        product(Y, 3, 1, "v", 5)
         gmask(1, 1)
-        product(Y, 3, 1, "v")
-        product(M1, 2, 0, "s")
-        product(M1, 2, 1, "s")
         addv(0)
+        product(M1, 2, 0, "s", 2)
+        product(M1, 2, 1, "s", 3)
+        product(M1, 3, 0, "s", 0)
         fused(1, 1)
-        product(M1, 3, 0, "s")
         fused(0, 3)
-        gmask(1, 2)
         addv(1)
-        product(M1, 3, 1, "s")
-        fused(1, 2)
+        gmask(1, 2)
+        product(M1, 3, 1, "s", 1)
         store(0, "s")
-        gmask(1, 3, 0, 256)
-        gmask(1, 3, 256, 512)
+        fused(1, 2)
         store(1, "v")
         addv(2)
+        gmask(1, 3, 0, 256)
+        gmask(1, 3, 256, 512)
         fused(1, 3, 0, 256)
         fused(1, 3, 256, 512)
         store(2, "s")

@@ -86,7 +86,7 @@ def tile_picked_zmodd_relu_po_kernel(tc, x_words, x_scales, w0, w1, w2, offs, ce
         def deal(i, h, t0, t1, eng):
             if grp[i] is None:
                 grp[i] = fresh("grp%d" % i, PACK * N, BF16)
-            walk = "p m j t" if eng == "v" else "p m t j"
+            walk = "p m t j" if eng == "g" else "p m j t"
             o = grp[i][:].rearrange("p (t m j) -> p t m j", t=PACK, j=PACK)[:, t0:t1, PIECES[i][h] // PACK : PIECES[i][h + 1] // PACK, :].rearrange("p t m j -> " + walk)
             s = raw[i][h].rearrange("p j (m t) -> p j m t", t=PACK)[:, :, :, t0:t1].rearrange("p j m t -> " + walk)
             if eng == "v":
@@ -104,7 +104,7 @@ def tile_picked_zmodd_relu_po_kernel(tc, x_words, x_scales, w0, w1, w2, offs, ce
             if eng == "v":
                 nc.vector.tensor_copy(out=o.rearrange("p m u j -> p m j u"), in_=s.rearrange("p m u j -> p m j u"))
             else:
-                nc.scalar.copy(out=o, in_=s)
+                nc.scalar.copy(out=o.rearrange("p m u j -> p m j u"), in_=s.rearrange("p m u j -> p m j u"))
 
         def unmix(step):
             if step == 0:

@@ -49,10 +49,10 @@ def tile_picked_zmodd_relu_po_kernel(tc, x_words, x_scales, w0, w1, w2, offs, ce
         mask = [[None] * PACK for d in range(2)]
         reuse = {}
         placed = {"raw0_0": 0, "raw0_1": T, "raw0_2": 3 * T // 2, "rows1_0": 3 * T // 4,
-                  "grp0": 3 * T, "grp2": 3 * T, "pr0_0": 12 * T - 1024, "pr0_1": 12 * T + 1024, "pr0_2": 12 * T + 3072,
+                  "grp0": 3 * T, "grp2": 3 * T, "pr0_0": 12 * T - 1024, "pr0_1": 12 * T + 1024,
                   "rows2_2": 6 * T, "fin0": 6 * T - 1024, "fin1": 6 * T + 1024, "fin2": 6 * T + 3072,
                   "raw1_0": 12 * T, "raw2_1": 12 * T,
-                  "rows2_1": 9 * T, "pr0_3": 9 * T}
+                  "rows2_1": 9 * T, "res": 10 * T - 1024, "rows0_2": 13 * T - 512, "rows1_1": 7 * T // 4}
         pr = [[None] * PACK for d in range(2)]
         fin = [None] * PACK
         og = keep.tile([P, V, PACK], BF16, name="og", align_bytes=64)
@@ -230,42 +230,41 @@ def tile_picked_zmodd_relu_po_kernel(tc, x_words, x_scales, w0, w1, w2, offs, ce
         deal(M1, 1, 0, 4, "g")
         product(M0, 0, 0, "v", 4)
         product(M0, 0, 1, "v", 5)
-        product(M0, 1, 0, "s", 0)
+        product(M0, 1, 0, "v", 6)
+        product(M0, 1, 1, "v", 7)
+        product(Y, 3, 0, "s", 0)
         gmixed()
         unmix(1)
-        product(M0, 1, 1, "s", 1)
         gmask(0, 0)
         gmask(0, 1)
-        product(Y, 0, 0, "v", 6)
-        product(Y, 0, 1, "v", 7)
-        product(Y, 1, 0, "v", 4)
-        product(Y, 1, 1, "v", 5)
-        product(Y, 2, 0, "v", 6)
-        product(Y, 2, 1, "v", 7)
+        product(Y, 0, 0, "v", 4)
+        product(Y, 0, 1, "v", 5)
+        product(Y, 1, 0, "v", 6)
+        product(Y, 1, 1, "v", 7)
         quant(M1, 0, 2)
         quant(M1, 2, 4)
         product(M1, 0, 0, "s", 2)
         product(M1, 0, 1, "s", 3)
         product(M1, 1, 0, "s", 0)
         fused(0, 0)
+        product(Y, 2, 0, "v", 4)
+        product(Y, 2, 1, "v", 5)
         gmask(1, 0)
         fused(0, 1)
         fused(0, 2)
         fused(1, 0)
-        hold("rows2_0", "rows0_3")
         product(M1, 1, 1, "s", 1)
-        product(Y, 3, 0, "s", 4)
-        product(Y, 3, 1, "v", 5)
+        product(Y, 3, 1, "s", 2)
         gmask(1, 1)
-        addv(0)
-        product(M1, 2, 0, "s", 2)
-        product(M1, 2, 1, "s", 3)
-        product(M1, 3, 0, "s", 0)
-        fused(1, 1)
         fused(0, 3)
+        product(M1, 2, 0, "s", 6)
+        product(M1, 2, 1, "s", 7)
+        product(M1, 3, 0, "s", 3)
+        fused(1, 1)
+        addv(0)
         addv(1)
         gmask(1, 2)
-        product(M1, 3, 1, "s", 1)
+        product(M1, 3, 1, "s", 0)
         store(0, "s")
         fused(1, 2)
         store(1, "v")

@@ -48,11 +48,11 @@ def tile_picked_zmodd_relu_po_kernel(tc, x_words, x_scales, w0, w1, w2, offs, ce
         rows = [[None] * PACK for i in range(3)]
         mask = [[None] * PACK for d in range(2)]
         reuse = {}
-        placed = {"raw0_0": 0, "raw0_1": T, "raw0_2": 3 * T // 2, "rows1_0": 3 * T // 4,
+        placed = {"raw0_0": 0, "raw0_1": T, "raw0_2": 3 * T // 2, "rows1_0": 0,
                   "grp0": 3 * T, "grp2": 3 * T, "pr0_0": 12 * T - 1024, "pr0_1": 12 * T + 1024,
                   "rows2_2": 6 * T, "fin0": 6 * T - 1024, "fin1": 6 * T + 1024, "fin2": 6 * T + 3072,
                   "raw1_0": 12 * T, "raw2_1": 12 * T,
-                  "rows2_1": 9 * T, "res": 10 * T - 1024, "rows0_2": 13 * T - 512, "rows1_1": 7 * T // 4}
+                  "rows2_1": 9 * T, "res": 10 * T - 1024, "rows1_1": 7 * T // 4}
         pr = [[None] * PACK for d in range(2)]
         fin = [None] * PACK
         og = keep.tile([P, V, PACK], BF16, name="og", align_bytes=64)
@@ -129,6 +129,12 @@ def tile_picked_zmodd_relu_po_kernel(tc, x_words, x_scales, w0, w1, w2, offs, ce
         def gwords(h):
             nc.vector.tensor_copy(gw[h][:], xw[:].indirect(offs_t[:, 32 * h : 32 * h + 32]))
 
+        def warm_up():
+            idle = psum.tile([P, HALF], F32, name="bank7")
+            for turn in range(2):
+                nc.tensor.matmul_mx(out=idle[:], lhsT=gw[0][:, 0:P].bitcast(FP8X4), lhsT_scale=gs0[:, 0:P],
+                                    rhs=gw[0][:].bitcast(FP8X4), rhs_scale=gs0[:, 0:HALF], start=True, stop=True)
+
         def product(i, t, h, eng, bank, a=0, b=HALF):
             acc = psum.tile([P, HALF], F32, name="bank%d" % bank)
             cols = slice(P * t, P * t + P)
@@ -190,7 +196,7 @@ def tile_picked_zmodd_relu_po_kernel(tc, x_words, x_scales, w0, w1, w2, offs, ce
         nc.vector.memset(warm[:], 0.0)
         nc.vector.memset(gs[:].bitcast(I32), 0)
         nc.scalar.activation(out=warm2[:], in_=warm[:], func=ACT.Sigmoid)
-        load_scales(nc.sync)
+        load_scales(nc.scalar)
         nc.sync.dma_start(offs_t[:], offs)
         nc.sync.dma_start(cen_t[:], cen)
         nc.sync.dma_start(pos1_t[:], pos1)
@@ -203,70 +209,73 @@ def tile_picked_zmodd_relu_po_kernel(tc, x_words, x_scales, w0, w1, w2, offs, ce
         load_w(Y, 1)
         load_w(Y, 2)
         gwords(0)
+        warm_up()
         gwords(1)
         deal_mixed(0, "s")
         deal(M0, 0, 0, 2, "s")
-        deal_mixed(1, "s")
+        deal(M0, 1, 0, 2, "s")
         hold("xw", "raw2_0")
         load_w(M1, 0)
         load_w(M1, 1)
         quant(M0, 2, 3)
-        deal(M0, 1, 0, 2, "v")
+        deal_mixed(1, "v")
         quant(M0, 3, 4)
         quant(M0, 0, 2)
         product(M0, 2, 0, "s", 0)
         product(M0, 2, 1, "s", 1)
         product(M0, 3, 0, "s", 2)
         deal(Y, 0, 0, 4, "v")
+        deal(Y, 1, 0, 4, "v")
+        deal(Y, 2, 0, 4, "g")
+        product(M0, 0, 0, "v", 4)
+        product(M0, 3, 1, "s", 3)
+        product(M0, 0, 1, "v", 5)
         gmask(0, 2)
         unmix(0)
-        product(M0, 3, 1, "s", 3)
-        deal(Y, 1, 0, 4, "v")
-        deal(Y, 2, 0, 2, "v")
-        deal(Y, 2, 2, 4, "v")
+        gmixed()
+        unmix(1)
         quant(Y, 0, 2)
         quant(Y, 2, 4)
         deal(M1, 0, 0, 4, "g")
         deal(M1, 1, 0, 4, "g")
-        product(M0, 0, 0, "v", 4)
-        product(M0, 0, 1, "v", 5)
         product(M0, 1, 0, "v", 6)
         product(M0, 1, 1, "v", 7)
-        product(Y, 3, 0, "s", 0)
-        gmixed()
-        unmix(1)
         gmask(0, 0)
-        gmask(0, 1)
         product(Y, 0, 0, "v", 4)
         product(Y, 0, 1, "v", 5)
+        gmask(0, 1)
+        product(Y, 3, 0, "s", 0)
         product(Y, 1, 0, "v", 6)
         product(Y, 1, 1, "v", 7)
+        product(Y, 2, 0, "v", 4)
+        product(Y, 2, 1, "s", 1)
+        product(Y, 3, 1, "s", 2, 0, 256)
         quant(M1, 0, 2)
         quant(M1, 2, 4)
-        product(M1, 0, 0, "s", 2)
-        product(M1, 0, 1, "s", 3)
-        product(M1, 1, 0, "s", 0)
+        product(M1, 0, 0, "s", 3)
+        product(M1, 0, 1, "s", 5)
+        product(M1, 1, 0, "s", 6)
         fused(0, 0)
-        product(Y, 2, 0, "v", 4)
-        product(Y, 2, 1, "v", 5)
+        product(Y, 3, 1, "v", 7, 256, 512)
         gmask(1, 0)
         fused(0, 1)
         fused(0, 2)
         fused(1, 0)
-        product(M1, 1, 1, "s", 1)
-        product(Y, 3, 1, "s", 2)
+        product(M1, 1, 1, "s", 0)
+        product(M1, 2, 0, "s", 1)
         gmask(1, 1)
         fused(0, 3)
-        product(M1, 2, 0, "s", 6)
-        product(M1, 2, 1, "s", 7)
-        product(M1, 3, 0, "s", 3)
+        product(M1, 2, 1, "s", 2)
+        product(M1, 3, 0, "s", 4)
         fused(1, 1)
         addv(0)
         addv(1)
-        gmask(1, 2)
-        product(M1, 3, 1, "s", 0)
+        gmask(1, 2, 0, 256)
+        gmask(1, 2, 256, 512)
+        product(M1, 3, 1, "s", 3)
         store(0, "s")
-        fused(1, 2)
+        fused(1, 2, 0, 256)
+        fused(1, 2, 256, 512)
         store(1, "v")
         addv(2)
         gmask(1, 3, 0, 256)

@@ -50,7 +50,7 @@ def tile_picked_zmodd_relu_po_kernel(tc, x_words, x_scales, w0, w1, w2, offs, ce
         reuse = {}
         placed = {"raw0_0": 0, "raw0_1": T, "raw0_2": 3 * T // 2, "rows1_0": 0,
                   "grp0": 3 * T, "grp2": 3 * T, "pr0_0": 12 * T - 1024, "pr0_1": 12 * T + 1024,
-                  "rows2_2": 6 * T, "fin0": 6 * T - 1024, "fin1": 6 * T + 1024, "fin2": 6 * T + 3072,
+                  "rows2_2": 6 * T, "fin1": 6 * T - 1024, "fin2": 6 * T + 1024, "pr1_1": 8 * T, "fin0": 8 * T,
                   "raw1_0": 12 * T, "raw2_1": 12 * T,
                   "rows2_1": 9 * T, "res": 10 * T - 1024, "rows1_1": 7 * T // 4}
         pr = [[None] * PACK for d in range(2)]
@@ -249,39 +249,41 @@ def tile_picked_zmodd_relu_po_kernel(tc, x_words, x_scales, w0, w1, w2, offs, ce
         product(Y, 1, 1, "v", 7)
         product(Y, 2, 0, "v", 4)
         product(Y, 2, 1, "s", 1)
-        product(Y, 3, 1, "s", 2, 0, 256)
+        product(Y, 3, 1, "s", 2)
         quant(M1, 0, 2)
         quant(M1, 2, 4)
         product(M1, 0, 0, "s", 3)
         product(M1, 0, 1, "s", 5)
         product(M1, 1, 0, "s", 6)
         fused(0, 0)
-        product(Y, 3, 1, "v", 7, 256, 512)
         gmask(1, 0)
         fused(0, 1)
         fused(0, 2)
         fused(1, 0)
         product(M1, 1, 1, "s", 0)
         product(M1, 2, 0, "s", 1)
-        gmask(1, 1)
+        gmask(1, 1, 0, 256)
+        gmask(1, 1, 256, 512)
         fused(0, 3)
         product(M1, 2, 1, "s", 2)
         product(M1, 3, 0, "s", 4)
-        fused(1, 1)
+        fused(1, 1, 0, 256)
+        fused(1, 1, 256, 512)
         addv(0)
         addv(1)
         gmask(1, 2, 0, 256)
-        gmask(1, 2, 256, 512)
         product(M1, 3, 1, "s", 3)
-        store(0, "s")
-        fused(1, 2, 0, 256)
-        fused(1, 2, 256, 512)
-        store(1, "v")
-        addv(2)
+        gmask(1, 2, 256, 512)
         gmask(1, 3, 0, 256)
         gmask(1, 3, 256, 512)
+        fused(1, 2, 0, 256)
+        store(0, "v")
+        addv(2, 0, 256)
+        fused(1, 2, 256, 512)
         fused(1, 3, 0, 256)
+        addv(2, 256, 512)
         fused(1, 3, 256, 512)
+        store(1, "s")
         store(2, "s")
         addv(3, 0, 256)
         addv(3, 256, 512)

@@ -213,23 +213,23 @@ def tile_picked_zmodd_relu_po_kernel(tc, x_words, x_scales, w0, w1, w2, offs, ce
         gwords(1)
         deal_mixed(0, "s")
         deal(M0, 0, 0, 2, "s")
-        deal(M0, 1, 0, 2, "s")
+        deal_mixed(1, "s")
         hold("xw", "raw2_0")
         load_w(M1, 0)
         load_w(M1, 1)
         quant(M0, 2, 3)
-        deal_mixed(1, "v")
-        quant(M0, 3, 4)
+        deal(M0, 1, 0, 2, "v")
         quant(M0, 0, 2)
+        quant(M0, 3, 4)
         product(M0, 2, 0, "s", 0)
         product(M0, 2, 1, "s", 1)
-        product(M0, 3, 0, "s", 2)
         deal(Y, 0, 0, 4, "v")
         deal(Y, 1, 0, 4, "v")
         deal(Y, 2, 0, 4, "g")
         product(M0, 0, 0, "v", 4)
-        product(M0, 3, 1, "s", 3)
+        product(M0, 3, 0, "s", 2)
         product(M0, 0, 1, "v", 5)
+        product(M0, 3, 1, "s", 3)
         gmask(0, 2)
         unmix(0)
         gmixed()

@@ -86,7 +86,7 @@ def tile_picked_zmodd_relu_po_kernel(tc, x_words, x_scales, w0, w1, w2, offs, ce
         def deal(i, h, t0, t1, eng):
             if grp[i] is None:
                 grp[i] = fresh("grp%d" % i, PACK * N, BF16)
-            walk = "p m t j" if eng == "g" else "p m j t"
+            walk = "p m t j" if i == M1 else "p m j t"
             o = grp[i][:].rearrange("p (t m j) -> p t m j", t=PACK, j=PACK)[:, t0:t1, PIECES[i][h] // PACK : PIECES[i][h + 1] // PACK, :].rearrange("p t m j -> " + walk)
             s = raw[i][h].rearrange("p j (m t) -> p j m t", t=PACK)[:, :, :, t0:t1].rearrange("p j m t -> " + walk)
             if eng == "v":
@@ -138,8 +138,9 @@ def tile_picked_zmodd_relu_po_kernel(tc, x_words, x_scales, w0, w1, w2, offs, ce
         def product(i, t, h, eng, bank, a=0, b=HALF):
             acc = psum.tile([P, HALF], F32, name="bank%d" % bank)
             cols = slice(P * t, P * t + P)
-            nc.tensor.matmul_mx(out=acc[:, 0 : b - a], lhsT=wc[i][:, cols].bitcast(FP8X4), lhsT_scale=ws[i][:, cols],
-                                rhs=gw[h][:, a:b].bitcast(FP8X4), rhs_scale=gs[:, HALF * h + a : HALF * h + b], start=True, stop=True)
+            for lo, hi in ((a, b),) if b - a != 384 else ((a, a + 256), (a + 256, b)):
+                nc.tensor.matmul_mx(out=acc[:, lo - a : hi - a], lhsT=wc[i][:, cols].bitcast(FP8X4), lhsT_scale=ws[i][:, cols],
+                                    rhs=gw[h][:, lo:hi].bitcast(FP8X4), rhs_scale=gs[:, HALF * h + lo : HALF * h + hi], start=True, stop=True)
             if rows[i][t] is None:
                 rows[i][t] = fresh("rows%d_%d" % (i, t), S)
             dst = rows[i][t][:, HALF * h + a : HALF * h + b]
@@ -249,13 +250,14 @@ def tile_picked_zmodd_relu_po_kernel(tc, x_words, x_scales, w0, w1, w2, offs, ce
         product(Y, 1, 1, "v", 7)
         product(Y, 2, 0, "v", 4)
         product(Y, 2, 1, "s", 1)
-        product(Y, 3, 1, "s", 2)
+        product(Y, 3, 1, "s", 2, 0, 384)
         quant(M1, 0, 2)
         quant(M1, 2, 4)
         product(M1, 0, 0, "s", 3)
         product(M1, 0, 1, "s", 5)
         product(M1, 1, 0, "s", 6)
         fused(0, 0)
+        product(Y, 3, 1, "v", 7, 384, 512)
         gmask(1, 0)
         fused(0, 1)
         fused(0, 2)

from contextlib import ExitStack

import concourse.mybir as mybir

K, T, S, V, N = 512, 4096, 1024, 512, 512
FLOPS = 3 * 2 * K * N * S

F32 = mybir.dt.float32
BF16 = mybir.dt.bfloat16
I32 = mybir.dt.int32
U32 = mybir.dt.uint32
U16 = mybir.dt.uint16
U8 = mybir.dt.uint8
FP8X4 = mybir.dt.float8_e4m3fn_x4
ACT = mybir.ActivationFunctionType
ALU = mybir.AluOpType

P = 128
PACK = 4
HALF = 512
BANKS = 8
Y, M0, M1 = 0, 1, 2
PIECES = ((0, 256, 384, 512), (0, 256, 512), (0, 256, 512))


def tile_picked_zmodd_relu_po_kernel(tc, x_words, x_scales, w0, w1, w2, offs, cen, pos1, pos2, out_0, out_1, out_2):
    nc = tc.nc
    with ExitStack() as ctx:
        keep = ctx.enter_context(tc.tile_pool(name="keep", bufs=1))
        shared = ctx.enter_context(tc.tile_pool(name="shared", bufs=1))
        psum = ctx.enter_context(tc.psum_pool(name="psum", bufs=1))

        offs_t = keep.tile([P, S // 16], U16, name="offs_t")
        cen_t = keep.tile([P, V // 16], U16, name="cen_t")
        pos1_t = keep.tile([P, V // 16], U16, name="pos1_t")
        pos2_t = keep.tile([P, V // 16], U16, name="pos2_t")
        xw = keep.tile([P, T], U32, name="xw", align_bytes=64)
        xs = shared.tile([P, T], U8, name="xs", align_bytes=64, offset=T - 64)
        raw = [[None] * 3 for i in range(3)]
        grp = [None] * 3
        wc = [keep.tile([P, N], U32, name="wc%d" % i, align_bytes=64) for i in range(3)]
        ws = [keep.tile([P, N], U8, name="ws%d" % i, align_bytes=64) for i in range(3)]
        warm = keep.tile([P, 1], F32, name="warm")
        warm2 = keep.tile([P, 1], F32, name="warm2")
        gs0 = keep.tile([P, S], U8, name="gs0", align_bytes=64)
        gs = keep.tile([P, S], U8, name="gs", align_bytes=64)
        gw = [keep.tile([P, HALF], U32, name="gw%d" % h, align_bytes=64) for h in range(2)]
        rows = [[None] * PACK for i in range(3)]
        mask = [[None] * PACK for d in range(2)]
        reuse = {}
        placed = {"raw0_0": 0, "raw0_1": T, "raw0_2": 3 * T // 2, "rows1_0": 0,
                  "grp0": 3 * T, "grp2": 3 * T, "pr0_0": 12 * T - 1024, "pr0_1": 12 * T + 1024,
                  "rows2_2": 6 * T, "fin1": 6 * T - 1024, "fin2": 6 * T + 1024, "pr1_1": 8 * T, "fin0": 8 * T,
                  "raw1_0": 12 * T, "raw2_1": 12 * T,
                  "rows2_1": 9 * T, "res": 10 * T - 1024, "rows1_1": 7 * T // 4}
        pr = [[None] * PACK for d in range(2)]
        fin = [None] * PACK
        og = keep.tile([P, V, PACK], BF16, name="og", align_bytes=64)
        oc = keep.tile([P, V], U32, name="oc", align_bytes=64)
        osc = keep.tile([P, V], U8, name="osc", align_bytes=64)
        out_rows = out_0.rearrange("(p t) c -> p t c", t=PACK)
        pos_t = (pos1_t, pos2_t)
        weights = (w0, w1, w2)
        mixed = []
        sums = []

        def hold(old, new):
            reuse[new] = reuse.get(old, old)

        def fresh(name, width, dt=F32):
            if name in placed:
                return shared.tile([P, width], dt, name=name, align_bytes=64, offset=placed[name])
            return keep.tile([P, width], dt, name=reuse.get(name, name), align_bytes=64)

        def load_w(i, h):
            c0, c1 = PIECES[i][h], PIECES[i][h + 1]
            raw[i][h] = fresh("raw%d_%d" % (i, h), PACK * (c1 - c0))[:].rearrange("p (j c) -> p j c", j=PACK)
            nc.sync.dma_start(out=raw[i][h], in_=weights[i].rearrange("(p j) c -> p j c", j=PACK)[:, :, c0:c1])

        def load_scales(eng):
            eng.dma_start(out=xs[16:32, :].bitcast(I32), in_=x_scales[0].bitcast(I32))

        def load_x():
            nc.sync.dma_start(out=xw[:].bitcast(I32), in_=x_words[0].rearrange("p n t -> p (n t)").bitcast(I32))

        def deal(i, h, t0, t1, eng):
            if grp[i] is None:
                grp[i] = fresh("grp%d" % i, PACK * N, BF16)
            walk = "p m t j" if i == M1 else "p m j t"
            o = grp[i][:].rearrange("p (t m j) -> p t m j", t=PACK, j=PACK)[:, t0:t1, PIECES[i][h] // PACK : PIECES[i][h + 1] // PACK, :].rearrange("p t m j -> " + walk)
            s = raw[i][h].rearrange("p j (m t) -> p j m t", t=PACK)[:, :, :, t0:t1].rearrange("p j m t -> " + walk)
            if eng == "v":
                nc.vector.tensor_copy(out=o, in_=s)
            elif eng == "g":
                nc.gpsimd.tensor_scalar(o, s, 1.0, 0.0, ALU.mult, ALU.add)
            else:
                nc.scalar.copy(out=o, in_=s)

        def deal_mixed(h, eng):
            if grp[M0] is None:
                grp[M0] = fresh("grp1", PACK * N, BF16)
            o = grp[M0][:, N * (2 + h) : N * (3 + h)].rearrange("p (u m j) -> p m u j", u=2, j=PACK)
            s = raw[M0][h].rearrange("p j (m t) -> p m t j", t=PACK)[:, :, 2:4, :]
            if eng == "v":
                nc.vector.tensor_copy(out=o.rearrange("p m u j -> p m j u"), in_=s.rearrange("p m u j -> p m j u"))
            else:
                nc.scalar.copy(out=o.rearrange("p m u j -> p m j u"), in_=s.rearrange("p m u j -> p m j u"))

        def unmix(step):
            if step == 0:
                mask[0][3] = fresh("mask0_3", V)
                nc.sync.dma_start(out=mask[0][3][0:64, :], in_=mask[0][2][64:P, :])
            else:
                nc.sync.dma_start(out=mask[0][3][64:P, :], in_=mixed[0][64:P, :])
                nc.sync.dma_start(out=mask[0][2][64:P, :], in_=mixed[0][0:64, :])

        def gmixed():
            mixed.append(fresh("mixed", V))
            nc.scalar.activation(out=mixed[0][:], in_=rows[M0][3][:].indirect(cen_t[:]), func=ACT.Sigmoid)

        def quant(i, t0, t1):
            nc.vector.quantize_mx(out=wc[i][:, P * t0 : P * t1].bitcast(FP8X4), scales=ws[i][:, P * t0 : P * t1], in_=grp[i][:, N * t0 : N * t1])

        def gscales(eng):
            nc.vector.tensor_copy(gs0[:], xs[:].indirect(offs_t[:]))
            for q in range(4):
                eng.dma_start(out=gs[32 * q : 32 * q + 4, :].bitcast(I32), in_=gs0[16 + 4 * q : 20 + 4 * q, :].bitcast(I32))

        def gwords(h):
            nc.vector.tensor_copy(gw[h][:], xw[:].indirect(offs_t[:, 32 * h : 32 * h + 32]))

        def warm_up():
            idle = psum.tile([P, HALF], F32, name="bank7")
            for turn in range(2):
                nc.tensor.matmul_mx(out=idle[:], lhsT=gw[0][:, 0:P].bitcast(FP8X4), lhsT_scale=gs0[:, 0:P],
                                    rhs=gw[0][:].bitcast(FP8X4), rhs_scale=gs0[:, 0:HALF], start=True, stop=True)

        def product(i, t, h, eng, bank, a=0, b=HALF):
            acc = psum.tile([P, HALF], F32, name="bank%d" % bank)
            cols = slice(P * t, P * t + P)
            for lo, hi in ((a, b),) if b - a != 384 else ((a, a + 256), (a + 256, b)):
                nc.tensor.matmul_mx(out=acc[:, lo - a : hi - a], lhsT=wc[i][:, cols].bitcast(FP8X4), lhsT_scale=ws[i][:, cols],
                                    rhs=gw[h][:, lo:hi].bitcast(FP8X4), rhs_scale=gs[:, HALF * h + lo : HALF * h + hi], start=True, stop=True)
            if rows[i][t] is None:
                rows[i][t] = fresh("rows%d_%d" % (i, t), S)
            dst = rows[i][t][:, HALF * h + a : HALF * h + b]
            if eng == "v":
                nc.vector.tensor_copy(out=dst, in_=acc[:, 0 : b - a])
            else:
                nc.scalar.copy(out=dst, in_=acc[:, 0 : b - a])

        def gmask(d, t, a=0, b=V):
            if mask[d][t] is None:
                mask[d][t] = fresh("mask%d_%d" % (d, t), V)
            nc.scalar.activation(out=mask[d][t][:, a:b], in_=rows[M0 + d][t][:].indirect(cen_t[:, a // 16 : b // 16]), func=ACT.Sigmoid)

        def fused(d, t, a=0, b=V):
            if pr[d][t] is None:
                pr[d][t] = fresh("pr%d_%d" % (d, t), V)
            nc.vector.tensor_tensor(pr[d][t][:, a:b], rows[Y][t][:].indirect(pos_t[d][:, a // 16 : b // 16]), mask[d][t][:, a:b], ALU.mult)

        def addv(t, a=0, b=V):
            if not sums:
                sums.append(fresh("res", PACK * V)[:].rearrange("p (t c) -> p t c", t=PACK))
            nc.vector.tensor_tensor(sums[0][:, t, a:b], pr[0][t][:, a:b], pr[1][t][:, a:b], ALU.add)

        def store(t, eng, a=0, b=V):
            if fin[t] is None:
                fin[t] = fresh("fin%d" % t, V)
            if eng == "s":
                nc.scalar.activation(out=fin[t][:, a:b], in_=sums[0][:, t, a:b], func=ACT.Relu)
            else:
                nc.vector.tensor_scalar_max(fin[t][:, a:b], sums[0][:, t, a:b], 0.0)
            if b == V:
                nc.sync.dma_start(out=out_rows[:, t, :], in_=fin[t][:])

        def weave(a, b, eng):
            o = og[:, a:b, :].rearrange("p (c i) t -> p c t i", i=PACK)
            s = sums[0][:, :, a:b].rearrange("p t (c i) -> p c t i", i=PACK)
            if eng == "s":
                nc.scalar.activation(out=o, in_=s, func=ACT.Relu)
            else:
                nc.vector.tensor_scalar_max(o, s, 0.0)

        def quantc(a, b):
            nc.vector.quantize_mx(out=oc[:, a:b].bitcast(FP8X4), scales=osc[:, a:b], in_=og[:, a:b, :].rearrange("p c t -> p (c t)"))
            nc.sync.dma_start(out=out_1[0, :, a:b, :].rearrange("p n t -> p (n t)").bitcast(I32), in_=oc[:, a:b].bitcast(I32))

        def scales_out():
            for q in range(4):
                eng = nc.scalar if q % 2 == 0 else nc.sync
                eng.dma_start(out=out_2[0, 4 * q : 4 * q + 4, :].bitcast(I32), in_=osc[32 * q : 32 * q + 4, :].bitcast(I32))

        nc.gpsimd.memset(xs[32:64, :].bitcast(I32), 0)
        nc.vector.memset(xs[0:16, :].bitcast(I32), 0)
        nc.vector.memset(xs[64:P, :].bitcast(I32), 0)
        nc.vector.memset(warm[:], 0.0)
        nc.vector.memset(gs[:].bitcast(I32), 0)
        nc.scalar.activation(out=warm2[:], in_=warm[:], func=ACT.Sigmoid)
        load_scales(nc.scalar)
        nc.sync.dma_start(offs_t[:], offs)
        nc.sync.dma_start(cen_t[:], cen)
        nc.sync.dma_start(pos1_t[:], pos1)
        load_x()
        load_w(M0, 0)
        load_w(M0, 1)
        nc.sync.dma_start(pos2_t[:], pos2)
        gscales(nc.sync)
        load_w(Y, 0)
        load_w(Y, 1)
        load_w(Y, 2)
        gwords(0)
        warm_up()
        gwords(1)
        deal_mixed(0, "s")
        deal(M0, 0, 0, 2, "s")
        deal_mixed(1, "s")
        hold("xw", "raw2_0")
        load_w(M1, 0)
        load_w(M1, 1)
        quant(M0, 2, 3)
        deal(M0, 1, 0, 2, "v")
        quant(M0, 0, 2)
        quant(M0, 3, 4)
        product(M0, 2, 0, "s", 0)
        product(M0, 2, 1, "s", 1)
        deal(Y, 0, 0, 4, "v")
        deal(Y, 1, 0, 4, "v")
        deal(Y, 2, 0, 4, "g")
        product(M0, 0, 0, "v", 4)
        product(M0, 3, 0, "s", 2)
        product(M0, 0, 1, "v", 5)
        product(M0, 3, 1, "s", 3)
        gmask(0, 2)
        unmix(0)
        gmixed()
        unmix(1)
        quant(Y, 0, 2)
        quant(Y, 2, 4)
        deal(M1, 0, 0, 4, "g")
        deal(M1, 1, 0, 4, "g")
        product(M0, 1, 0, "v", 6)
        product(M0, 1, 1, "v", 7)
        gmask(0, 0)
        product(Y, 0, 0, "v", 4)
        product(Y, 0, 1, "v", 5)
        gmask(0, 1)
        product(Y, 3, 0, "s", 0)
        product(Y, 1, 0, "v", 6)
        product(Y, 1, 1, "v", 7)
        product(Y, 2, 0, "v", 4)
        product(Y, 2, 1, "s", 1)
        product(Y, 3, 1, "s", 2, 0, 384)
        quant(M1, 0, 2)
        quant(M1, 2, 4)
        product(M1, 0, 0, "s", 3)
        product(M1, 0, 1, "s", 5)
        product(M1, 1, 0, "s", 6)
        fused(0, 0)
        product(Y, 3, 1, "v", 7, 384, 512)
        gmask(1, 0)
        fused(0, 1)
        fused(0, 2)
        fused(1, 0)
        product(M1, 1, 1, "s", 0)
        product(M1, 2, 0, "s", 1)
        gmask(1, 1, 0, 256)
        gmask(1, 1, 256, 512)
        fused(0, 3)
        product(M1, 2, 1, "s", 2)
        product(M1, 3, 0, "s", 4)
        fused(1, 1, 0, 256)
        fused(1, 1, 256, 512)
        addv(0)
        addv(1)
        gmask(1, 2, 0, 256)
        product(M1, 3, 1, "s", 3)
        gmask(1, 2, 256, 512)
        gmask(1, 3, 0, 256)
        gmask(1, 3, 256, 512)
        fused(1, 2, 0, 256)
        store(0, "v")
        addv(2, 0, 256)
        fused(1, 2, 256, 512)
        fused(1, 3, 0, 256)
        addv(2, 256, 512)
        fused(1, 3, 256, 512)
        store(1, "s")
        store(2, "s")
        addv(3, 0, 256)
        addv(3, 256, 512)
        store(3, "s", 0, 256)
        store(3, "s", 256, 512)
        weave(0, 256, "v")
        weave(256, 512, "v")
        quantc(0, 256)
        quantc(256, 512)
        scales_out()
